import numpy as np
import ml_dtypes


def mxq(x, axis, fmt="e4m3"):
    dtype, down = {"e4m3": (ml_dtypes.float8_e4m3fn, 7), "e5m2": (ml_dtypes.float8_e5m2, 14)}[fmt]
    v = np.moveaxis(np.asarray(x, np.float32).astype(ml_dtypes.bfloat16).astype(np.float64), axis, -1)
    blocks = v.reshape(v.shape[:-1] + (-1, 32))
    amax = np.abs(blocks).max(-1, keepdims=True)
    byte = np.maximum(np.where(amax > 0, np.frexp(amax)[1] - 1 + 127, 0) - down, 1)
    scale = np.exp2(byte - 127.0)
    codes = (blocks / scale).astype(np.float32).astype(dtype).astype(np.float64)
    return np.moveaxis((codes * scale).reshape(v.shape), -1, axis)


WIDE = False


def mx_kscale(k):
    if not WIDE:
        return np.ones(k)
    levels = np.array([10, -10, 5, -5, 0])
    if k % 512:
        return np.exp2(np.random.permutation(np.resize(levels, k // 32))).repeat(32)
    a = np.empty((k // 512, 16))
    for p in range(k // 512):
        a[p, :8] = np.random.permutation(np.resize(levels, 8))
        for g in range(8):
            far = levels[np.abs(levels - a[p, g]) >= 10]
            a[p, g + 8] = far[np.random.randint(len(far))]
    return np.exp2(a.ravel()).repeat(32)


def f64(x):
    return np.asarray(x).astype(np.float64)


def striped(idx):
    return np.tile(np.asarray(idx).reshape(-1, 16).T, (8, 1)).astype(np.uint16)


def unstriped(offs):
    return offs[:16].T.reshape(-1).astype(np.int64)


E2M1 = np.array([0.0, 0.5, 1.0, 1.5, 2.0, 3.0, 4.0, 6.0, -0.0, -0.5, -1.0, -1.5, -2.0, -3.0, -4.0, -6.0])


def pack_weight(w, fmt):
    k, n = w.shape
    w = f64(np.asarray(w, np.float32).astype(ml_dtypes.bfloat16)).reshape(k // 32, 32, n)
    amax = np.abs(w).max(1)
    if fmt == "e4m3":
        byte = np.frexp(amax)[1] - 1 + 127 - 7
    else:
        mant, ex = np.frexp(amax / 6.0)
        byte = np.where(mant > 0.5, ex, ex - 1) + 127
    byte = np.clip(np.where(amax > 0, byte, 1), 1, 254)
    scaled = (w * np.exp2(127.0 - byte)[:, None, :]).reshape(k, n).astype(np.float32)
    by_word = np.ascontiguousarray(scaled.reshape(k // 512, 128, 4, n).transpose(0, 1, 3, 2))
    if fmt == "e4m3":
        words = by_word.astype(ml_dtypes.float8_e4m3fn).view(np.uint8)
    else:
        c = by_word.astype(ml_dtypes.float4_e2m1fn).view(np.uint8) & 0xF
        words = (c[..., 0::2] | (c[..., 1::2] << 4)).reshape(k // 512, 128, 2 * n)
    return np.ascontiguousarray(words), np.ascontiguousarray(byte.astype(np.uint8).reshape(k // 512, 16, n))


def unpack_weight(words, scales, fmt):
    g, _, n = scales.shape
    words = np.ascontiguousarray(words).reshape(g, 128, n, -1)
    if fmt == "e4m3":
        vals = words.view(ml_dtypes.float8_e4m3fn).astype(np.float64)
    else:
        nib = np.empty((g, 128, n, 4), np.uint8)
        nib[..., 0::2] = words & 0xF
        nib[..., 1::2] = words >> 4
        vals = E2M1[nib]
    vals = vals * np.repeat(np.exp2(scales.astype(np.float64) - 127.0), 8, axis=1)[..., None]
    return vals.transpose(0, 1, 3, 2).reshape(g * 512, n)


def bf(x):
    return np.asarray(x, np.float32).astype(ml_dtypes.bfloat16)


def planes(Y):
    r, m = Y.shape
    b = f64(bf(Y)).reshape(r // 32, 32, m)
    amax = np.abs(b).max(1)
    byte = np.clip(np.where(amax > 0, np.frexp(amax)[1] - 1 + 127 - 7, 1), 1, 254)
    codes = (b * np.exp2(127.0 - byte)[:, None, :]).reshape(r, m).astype(np.float32).astype(ml_dtypes.float8_e4m3fn).view(np.uint8)
    words = codes.reshape(r // 512, 128, 4, m).transpose(0, 1, 3, 2)
    return np.ascontiguousarray(words), np.ascontiguousarray(byte.astype(np.uint8).reshape(r // 512, 16, m))


B, N, T, D, NQ = 1, 512, 2048, 512, 512


def setup_inputs():
    n = np.random.standard_normal
    idx = np.sort(np.random.permutation(T)[:B * N].reshape(B, N), axis=1).reshape(-1)
    s = mx_kscale(D)[:, None]
    kp = pack_weight(n((D, T)) / s, "e4m3")
    return {
        "qT": (n((B, D, NQ)) * s * (1.00 / np.sqrt(D))).astype(np.float32),
        "k_words": kp[0],
        "k_scales": kp[1],
        "offs": striped(idx),
    }


def reference(qT, k_words, k_scales, offs):
    idx = unstriped(offs)
    pick = lambda x, which: x[:, which].reshape(x.shape[0], B, -1).transpose(1, 0, 2)
    k = unpack_weight(k_words, k_scales, "e4m3")
    kg = pick(k, idx)
    qq = mxq(f64(qT), 1, "e4m3")
    a = kg.transpose(0, 2, 1) @ qq
    y = np.square(np.maximum(a, 0.0))
    Y = y[0]
    words, scales = planes(Y)
    return Y, words, scales

@@ -1,0 +1,128 @@
+from contextlib import ExitStack
+
+import concourse.mybir as mybir
+
+F32 = mybir.dt.float32
+BF16 = mybir.dt.bfloat16
+I32 = mybir.dt.int32
+U32 = mybir.dt.uint32
+U16 = mybir.dt.uint16
+U8 = mybir.dt.uint8
+FP8X4 = mybir.dt.float8_e4m3fn_x4
+ACT = mybir.ActivationFunctionType
+ALU = mybir.AluOpType
+
+P = 128
+PACK = 4
+D, T, N, NQ = 512, 2048, 512, 512
+CHUNK = 128
+CHUNKS = NQ // CHUNK
+HALF = NQ // 2
+FLOPS = 2 * D * N * NQ
+
+
+def weave(copy, dst, src):
+    copy(dst.rearrange("p (c i) t -> p c t i", i=4), src.rearrange("p t (c i) -> p c t i", i=4))
+
+
+def tile_attend_plh_relu2_srt_kernel(tc, qT, k_words, k_scales, offs, out_0, out_1, out_2):
+    nc = tc.nc
+    with ExitStack() as ctx:
+        sb = ctx.enter_context(tc.tile_pool(name="sb", bufs=1))
+        ps = ctx.enter_context(tc.psum_pool(name="ps", bufs=1))
+
+        q_rows = qT[0].rearrange("(p t) q -> p t q", t=PACK)
+        widths = [256, 128, 128]
+        starts = [sum(widths[:i]) for i in range(len(widths))]
+        q_raw = [sb.tile([P, PACK, w], F32, name="q_raw%d" % i, align_bytes=64) for i, w in enumerate(widths)]
+        offsets = sb.tile([P, N // 16], U16, name="offsets", align_bytes=64)
+        pool_words = sb.tile([P, T], U32, name="pool_words", align_bytes=64)
+        pool_scales = sb.tile([P, T], U8, name="pool_scales", tag="scale_bytes", align_bytes=64)
+
+        nc.vector.memset(pool_scales[:].bitcast(I32), 0)
+        nc.sync.dma_start(out=q_raw[0][:], in_=q_rows[:, :, 0 : widths[0]])
+        nc.sync.dma_start(offsets[:], offs)
+        for quad in range(4):
+            queue = nc.sync if quad % 2 == 0 else nc.scalar
+            queue.dma_start(out=pool_scales[32 * quad : 32 * quad + 4, :].bitcast(I32),
+                            in_=k_scales[0, 4 * quad : 4 * quad + 4, :].bitcast(I32))
+        nc.sync.dma_start(out=pool_words[:].bitcast(I32),
+                          in_=k_words[0].rearrange("p n t -> p (n t)").bitcast(I32))
+        for i in range(1, len(widths)):
+            nc.sync.dma_start(out=q_raw[i][:], in_=q_rows[:, :, starts[i] : starts[i] + widths[i]])
+
+        q_bf = [sb.tile([P, w, PACK], BF16, name="q_bf%d" % i, align_bytes=64) for i, w in enumerate(widths)]
+        q_codes = [sb.tile([P, w], U32, name="q_codes%d" % i, align_bytes=64) for i, w in enumerate(widths)]
+        q_scales = []
+
+        def quantize_q(i):
+            tag = "scale_bytes" if i == 0 else "q_scales%d" % i
+            q_scales.append(sb.tile([P, widths[i]], U8, name="q_scales%d" % i, tag=tag, align_bytes=64))
+            nc.vector.quantize_mx(out=q_codes[i][:].bitcast(FP8X4), scales=q_scales[i][:],
+                                  in_=q_bf[i][:].rearrange("p c t -> p (c t)"))
+
+        weave(nc.scalar.copy, q_bf[0][:], q_raw[0][:])
+
+        listed_scales = sb.tile([P, N], U8, name="listed_scales", align_bytes=64)
+        k_sc = sb.tile([P, N], U8, name="k_sc", align_bytes=64)
+        k_w = sb.tile([P, N], U32, name="k_w", align_bytes=64)
+        nc.vector.tensor_copy(listed_scales[:], pool_scales[:].indirect(offsets[:]))
+        quantize_q(0)
+        nc.vector.tensor_copy(k_sc[:].rearrange("p (r s) -> p r s", r=PACK),
+                              listed_scales[:].rearrange("p (s r) -> p r s", r=PACK))
+        nc.vector.tensor_copy(k_w[:].rearrange("p (r s) -> p s r", r=PACK), pool_words[:].indirect(offsets[:]))
+
+        for i in range(1, len(widths)):
+            weave(nc.vector.tensor_copy if i in (2,) else nc.scalar.copy, q_bf[i][:], q_raw[i][:])
+            quantize_q(i)
+
+        y_rows = out_0.rearrange("(p u) q -> p u q", u=PACK)
+        y_words_out = out_1[0].rearrange("p q u -> p (q u)").bitcast(I32)
+        y_codes = sb.tile([P, NQ], U32, name="y_codes", align_bytes=64)
+        y_scales = sb.tile([P, NQ], U8, name="y_scales", align_bytes=64)
+        acc = [ps.tile([P, PACK, CHUNK], F32, name="acc%d" % c) for c in range(CHUNKS)]
+        pos = [sb.tile([P, PACK, CHUNK], F32, name="pos%d" % c, align_bytes=64) for c in range(CHUNKS)]
+        y = [sb.tile([P, PACK, CHUNK], F32, name="y%d" % c, align_bytes=64) for c in range(CHUNKS)]
+        y_bf = [sb.tile([P, CHUNK, PACK], BF16, name="y_bf%d" % c, align_bytes=64) for c in range(CHUNKS)]
+
+        def multiply(c):
+            h = max(i for i in range(len(widths)) if starts[i] <= c * CHUNK)
+            lo = c * CHUNK - starts[h]
+            for r in range(PACK):
+                slots = slice(r * P, (r + 1) * P)
+                nc.tensor.matmul_mx(out=acc[c][:, r, :], lhsT=k_w[:, slots].bitcast(FP8X4), lhsT_scale=k_sc[:, slots],
+                                    rhs=q_codes[h][:, lo : lo + CHUNK].bitcast(FP8X4),
+                                    rhs_scale=q_scales[h][:, lo : lo + CHUNK], start=True, stop=True)
+
+        def relu(c):
+            nc.scalar.activation(pos[c][:], acc[c][:], ACT.Relu)
+
+        def square(c):
+            split = (4, 4, 2, 0)[c]
+            if split > 0:
+                nc.vector.tensor_tensor(y[c][:, :split, :], pos[c][:, :split, :], pos[c][:, :split, :], ALU.mult)
+            if split < PACK:
+                nc.scalar.activation(y[c][:, split:, :], pos[c][:, split:, :], ACT.Square)
+            nc.sync.dma_start(out=y_rows[:, :, c * CHUNK : (c + 1) * CHUNK], in_=y[c][:])
+
+        def round_y(c):
+            weave(nc.vector.tensor_copy, y_bf[c][:], y[c][:])
+
+        def quantize_y(c):
+            cols = slice(c * CHUNK, (c + 1) * CHUNK)
+            nc.vector.quantize_mx(out=y_codes[:, cols].bitcast(FP8X4), scales=y_scales[:, cols],
+                                  in_=y_bf[c][:].rearrange("p c t -> p (c t)"))
+            if c >= 2:
+                cols = slice(0 if c == 2 else c * CHUNK, (c + 1) * CHUNK)
+                nc.sync.dma_start(out=y_words_out[:, cols], in_=y_codes[:, cols].bitcast(I32))
+
+        stages = [multiply, relu, square, round_y, quantize_y]
+        for step in range(CHUNKS + len(stages) - 1):
+            for depth in reversed(range(len(stages))):
+                if 0 <= step - depth < CHUNKS:
+                    stages[depth](step - depth)
+
+        for quad in range(4):
+            queue = nc.scalar if quad % 2 == 0 else nc.sync
+            queue.dma_start(out=out_2[0, 4 * quad : 4 * quad + 4, :].bitcast(I32),
+                            in_=y_scales[32 * quad : 32 * quad + 4, :].bitcast(I32))

@@ -17,7 +17,9 @@ PACK = 4
 D, T, N, NQ = 512, 2048, 512, 512
 CHUNK = 128
 CHUNKS = NQ // CHUNK
-HALF = NQ // 2
+EARLY = N // 2
+PREFIX = T - (N - EARLY)
+VECTOR_SQUARES = (2, 4, 2, 0)
 FLOPS = 2 * D * N * NQ
 
 
@@ -31,37 +33,41 @@ def tile_attend_plh_relu2_srt_kernel(tc, qT, k_words, k_scales, offs, out_0, out
         sb = ctx.enter_context(tc.tile_pool(name="sb", bufs=1))
         ps = ctx.enter_context(tc.psum_pool(name="ps", bufs=1))
 
+        def cols(c, n=1):
+            return slice(c * CHUNK, (c + n) * CHUNK)
+
         q_rows = qT[0].rearrange("(p t) q -> p t q", t=PACK)
-        widths = [256, 128, 128]
-        starts = [sum(widths[:i]) for i in range(len(widths))]
-        q_raw = [sb.tile([P, PACK, w], F32, name="q_raw%d" % i, align_bytes=64) for i, w in enumerate(widths)]
+        words_in = k_words[0].rearrange("p n t -> p (n t)").bitcast(I32)
+        q_raw = [sb.tile([P, PACK, CHUNK], F32, name="q_raw%d" % c, tag="f32_%d" % c, align_bytes=64)
+                 for c in range(CHUNKS)]
         offsets = sb.tile([P, N // 16], U16, name="offsets", align_bytes=64)
         pool_words = sb.tile([P, T], U32, name="pool_words", align_bytes=64)
         pool_scales = sb.tile([P, T], U8, name="pool_scales", tag="scale_bytes", align_bytes=64)
 
         nc.vector.memset(pool_scales[:].bitcast(I32), 0)
-        nc.sync.dma_start(out=q_raw[0][:], in_=q_rows[:, :, 0 : widths[0]])
+        nc.sync.dma_start(out=q_raw[0][:], in_=q_rows[:, :, cols(0)])
         nc.sync.dma_start(offsets[:], offs)
         for quad in range(4):
             queue = nc.sync if quad % 2 == 0 else nc.scalar
             queue.dma_start(out=pool_scales[32 * quad : 32 * quad + 4, :].bitcast(I32),
                             in_=k_scales[0, 4 * quad : 4 * quad + 4, :].bitcast(I32))
-        nc.sync.dma_start(out=pool_words[:].bitcast(I32),
-                          in_=k_words[0].rearrange("p n t -> p (n t)").bitcast(I32))
-        for i in range(1, len(widths)):
-            nc.sync.dma_start(out=q_raw[i][:], in_=q_rows[:, :, starts[i] : starts[i] + widths[i]])
+        nc.sync.dma_start(out=pool_words[:, :PREFIX].bitcast(I32), in_=words_in[:, :PREFIX])
+        nc.sync.dma_start(out=pool_words[:, PREFIX:].bitcast(I32), in_=words_in[:, PREFIX:])
+        for c in range(1, CHUNKS):
+            nc.sync.dma_start(out=q_raw[c][:], in_=q_rows[:, :, cols(c)])
 
-        q_bf = [sb.tile([P, w, PACK], BF16, name="q_bf%d" % i, align_bytes=64) for i, w in enumerate(widths)]
-        q_codes = [sb.tile([P, w], U32, name="q_codes%d" % i, align_bytes=64) for i, w in enumerate(widths)]
+        q_bf = [sb.tile([P, CHUNK, PACK], BF16, name="q_bf%d" % c, align_bytes=64) for c in range(CHUNKS)]
+        q_codes = [sb.tile([P, CHUNK], U32, name="q_codes%d" % c, align_bytes=64) for c in range(CHUNKS)]
         q_scales = []
 
-        def quantize_q(i):
-            tag = "scale_bytes" if i == 0 else "q_scales%d" % i
-            q_scales.append(sb.tile([P, widths[i]], U8, name="q_scales%d" % i, tag=tag, align_bytes=64))
-            nc.vector.quantize_mx(out=q_codes[i][:].bitcast(FP8X4), scales=q_scales[i][:],
-                                  in_=q_bf[i][:].rearrange("p c t -> p (c t)"))
+        def quantize_q(c):
+            tag = "scale_bytes" if c == 0 else "q_scales%d" % c
+            q_scales.append(sb.tile([P, CHUNK], U8, name="q_scales%d" % c, tag=tag, align_bytes=64))
+            nc.vector.quantize_mx(out=q_codes[c][:].bitcast(FP8X4), scales=q_scales[c][:],
+                                  in_=q_bf[c][:].rearrange("p c t -> p (c t)"))
 
-        weave(nc.scalar.copy, q_bf[0][:], q_raw[0][:])
+        for c in range(CHUNKS):
+            weave(nc.scalar.copy, q_bf[c][:], q_raw[c][:])
 
         listed_scales = sb.tile([P, N], U8, name="listed_scales", align_bytes=64)
         k_sc = sb.tile([P, N], U8, name="k_sc", align_bytes=64)
@@ -70,55 +76,61 @@ def tile_attend_plh_relu2_srt_kernel(tc, qT, k_words, k_scales, offs, out_0, out
         quantize_q(0)
         nc.vector.tensor_copy(k_sc[:].rearrange("p (r s) -> p r s", r=PACK),
                               listed_scales[:].rearrange("p (s r) -> p r s", r=PACK))
-        nc.vector.tensor_copy(k_w[:].rearrange("p (r s) -> p s r", r=PACK), pool_words[:].indirect(offsets[:]))
-
-        for i in range(1, len(widths)):
-            weave(nc.vector.tensor_copy if i in (2,) else nc.scalar.copy, q_bf[i][:], q_raw[i][:])
-            quantize_q(i)
+        dealt = k_w[:].rearrange("p (r s) -> p s r", r=PACK)
+        nc.vector.tensor_copy(dealt[:, : EARLY // PACK, :], pool_words[:, :PREFIX].indirect(offsets[:, : EARLY // 16]))
+        nc.vector.tensor_copy(dealt[:, EARLY // PACK :, :], pool_words[:].indirect(offsets[:, EARLY // 16 :]))
+        for c in range(1, CHUNKS):
+            quantize_q(c)
 
         y_rows = out_0.rearrange("(p u) q -> p u q", u=PACK)
         y_words_out = out_1[0].rearrange("p q u -> p (q u)").bitcast(I32)
         y_codes = sb.tile([P, NQ], U32, name="y_codes", align_bytes=64)
         y_scales = sb.tile([P, NQ], U8, name="y_scales", align_bytes=64)
-        acc = [ps.tile([P, PACK, CHUNK], F32, name="acc%d" % c) for c in range(CHUNKS)]
-        pos = [sb.tile([P, PACK, CHUNK], F32, name="pos%d" % c, align_bytes=64) for c in range(CHUNKS)]
+        acc = [[ps.tile([P, 2, CHUNK], F32, name="acc%d_%d" % (c, h)) for h in range(2)] if c in (0,) else
+               [ps.tile([P, PACK, CHUNK], F32, name="acc%d" % c)] for c in range(CHUNKS)]
+        pos = []
         y = [sb.tile([P, PACK, CHUNK], F32, name="y%d" % c, align_bytes=64) for c in range(CHUNKS)]
         y_bf = [sb.tile([P, CHUNK, PACK], BF16, name="y_bf%d" % c, align_bytes=64) for c in range(CHUNKS)]
 
         def multiply(c):
-            h = max(i for i in range(len(widths)) if starts[i] <= c * CHUNK)
-            lo = c * CHUNK - starts[h]
+            per_bank = PACK // len(acc[c])
             for r in range(PACK):
                 slots = slice(r * P, (r + 1) * P)
-                nc.tensor.matmul_mx(out=acc[c][:, r, :], lhsT=k_w[:, slots].bitcast(FP8X4), lhsT_scale=k_sc[:, slots],
-                                    rhs=q_codes[h][:, lo : lo + CHUNK].bitcast(FP8X4),
-                                    rhs_scale=q_scales[h][:, lo : lo + CHUNK], start=True, stop=True)
+                nc.tensor.matmul_mx(out=acc[c][r // per_bank][:, r % per_bank, :], lhsT=k_w[:, slots].bitcast(FP8X4),
+                                    lhsT_scale=k_sc[:, slots], rhs=q_codes[c][:].bitcast(FP8X4),
+                                    rhs_scale=q_scales[c][:], start=True, stop=True)
 
         def relu(c):
-            nc.scalar.activation(pos[c][:], acc[c][:], ACT.Relu)
+            pos.append(sb.tile([P, PACK, CHUNK], F32, name="pos%d" % c, tag="f32_%d" % (CHUNKS - 1 - c), align_bytes=64))
+            if len(acc[c]) == 1:
+                nc.scalar.activation(pos[c][:], acc[c][0][:], ACT.Relu)
+            else:
+                nc.scalar.activation(pos[c][:, 2:, :], acc[c][1][:], ACT.Relu)
+                nc.vector.tensor_scalar(pos[c][:, :2, :], acc[c][0][:], 0.0, None, ALU.max)
 
         def square(c):
-            split = (4, 4, 2, 0)[c]
+            split = VECTOR_SQUARES[c]
             if split > 0:
                 nc.vector.tensor_tensor(y[c][:, :split, :], pos[c][:, :split, :], pos[c][:, :split, :], ALU.mult)
             if split < PACK:
                 nc.scalar.activation(y[c][:, split:, :], pos[c][:, split:, :], ACT.Square)
-            nc.sync.dma_start(out=y_rows[:, :, c * CHUNK : (c + 1) * CHUNK], in_=y[c][:])
+            nc.sync.dma_start(out=y_rows[:, :, cols(c)], in_=y[c][:])
 
         def round_y(c):
             weave(nc.vector.tensor_copy, y_bf[c][:], y[c][:])
 
         def quantize_y(c):
-            cols = slice(c * CHUNK, (c + 1) * CHUNK)
-            nc.vector.quantize_mx(out=y_codes[:, cols].bitcast(FP8X4), scales=y_scales[:, cols],
+            nc.vector.quantize_mx(out=y_codes[:, cols(c)].bitcast(FP8X4), scales=y_scales[:, cols(c)],
                                   in_=y_bf[c][:].rearrange("p c t -> p (c t)"))
-            if c >= 2:
-                cols = slice(0 if c == 2 else c * CHUNK, (c + 1) * CHUNK)
-                nc.sync.dma_start(out=y_words_out[:, cols], in_=y_codes[:, cols].bitcast(I32))
+            if c == 1:
+                nc.sync.dma_start(out=y_words_out[:, cols(0, c + 1)], in_=y_codes[:, cols(0, c + 1)].bitcast(I32))
+            if c == CHUNKS - 1:
+                rest = cols(1 + 1, CHUNKS - 1 - 1)
+                nc.sync.dma_start(out=y_words_out[:, rest], in_=y_codes[:, rest].bitcast(I32))
 
         stages = [multiply, relu, square, round_y, quantize_y]
         for step in range(CHUNKS + len(stages) - 1):
-            for depth in reversed(range(len(stages))):
+            for depth in range(len(stages)):
                 if 0 <= step - depth < CHUNKS:
                     stages[depth](step - depth)
 

@@ -20,6 +20,7 @@ CHUNKS = NQ // CHUNK
 EARLY = N // 2
 PREFIX = T - (N - EARLY)
 VECTOR_SQUARES = (2, 4, 2, 0)
+Q_LOADS = [(0, 2), (2, 1), (3, 1)]
 FLOPS = 2 * D * N * NQ
 
 
@@ -38,35 +39,34 @@ def tile_attend_plh_relu2_srt_kernel(tc, qT, k_words, k_scales, offs, out_0, out
 
         q_rows = qT[0].rearrange("(p t) q -> p t q", t=PACK)
         words_in = k_words[0].rearrange("p n t -> p (n t)").bitcast(I32)
-        q_raw = [sb.tile([P, PACK, CHUNK], F32, name="q_raw%d" % c, tag="f32_%d" % c, align_bytes=64)
-                 for c in range(CHUNKS)]
+        q_raw = [sb.tile([P, PACK, n * CHUNK], F32, name="q_raw%d" % c, tag="f32_%d" % c, align_bytes=64)
+                 for c, n in Q_LOADS]
         offsets = sb.tile([P, N // 16], U16, name="offsets", align_bytes=64)
         pool_words = sb.tile([P, T], U32, name="pool_words", align_bytes=64)
         pool_scales = sb.tile([P, T], U8, name="pool_scales", tag="scale_bytes", align_bytes=64)
 
         nc.vector.memset(pool_scales[:].bitcast(I32), 0)
-        nc.sync.dma_start(out=q_raw[0][:], in_=q_rows[:, :, cols(0)])
+        nc.sync.dma_start(out=q_raw[0][:], in_=q_rows[:, :, cols(*Q_LOADS[0])])
         nc.sync.dma_start(offsets[:], offs)
         for quad in range(4):
-            queue = nc.sync if quad % 2 == 0 else nc.scalar
-            queue.dma_start(out=pool_scales[32 * quad : 32 * quad + 4, :].bitcast(I32),
-                            in_=k_scales[0, 4 * quad : 4 * quad + 4, :].bitcast(I32))
+            nc.sync.dma_start(out=pool_scales[32 * quad : 32 * quad + 4, :].bitcast(I32),
+                              in_=k_scales[0, 4 * quad : 4 * quad + 4, :].bitcast(I32))
         nc.sync.dma_start(out=pool_words[:, :PREFIX].bitcast(I32), in_=words_in[:, :PREFIX])
         nc.sync.dma_start(out=pool_words[:, PREFIX:].bitcast(I32), in_=words_in[:, PREFIX:])
-        for c in range(1, CHUNKS):
-            nc.sync.dma_start(out=q_raw[c][:], in_=q_rows[:, :, cols(c)])
+        for i in range(1, len(Q_LOADS)):
+            nc.sync.dma_start(out=q_raw[i][:], in_=q_rows[:, :, cols(*Q_LOADS[i])])
 
-        q_bf = [sb.tile([P, CHUNK, PACK], BF16, name="q_bf%d" % c, align_bytes=64) for c in range(CHUNKS)]
-        q_codes = [sb.tile([P, CHUNK], U32, name="q_codes%d" % c, align_bytes=64) for c in range(CHUNKS)]
+        q_bf = [sb.tile([P, n * CHUNK, PACK], BF16, name="q_bf%d" % c, align_bytes=64) for c, n in Q_LOADS]
+        q_codes = [sb.tile([P, n * CHUNK], U32, name="q_codes%d" % c, align_bytes=64) for c, n in Q_LOADS]
         q_scales = []
 
         def quantize_q(c):
             tag = "scale_bytes" if c == 0 else "q_scales%d" % c
-            q_scales.append(sb.tile([P, CHUNK], U8, name="q_scales%d" % c, tag=tag, align_bytes=64))
+            q_scales.append(sb.tile([P, Q_LOADS[c][1] * CHUNK], U8, name="q_scales%d" % c, tag=tag, align_bytes=64))
             nc.vector.quantize_mx(out=q_codes[c][:].bitcast(FP8X4), scales=q_scales[c][:],
                                   in_=q_bf[c][:].rearrange("p c t -> p (c t)"))
 
-        for c in range(CHUNKS):
+        for c in range(len(Q_LOADS)):
             weave(nc.scalar.copy, q_bf[c][:], q_raw[c][:])
 
         listed_scales = sb.tile([P, N], U8, name="listed_scales", align_bytes=64)
@@ -79,7 +79,7 @@ def tile_attend_plh_relu2_srt_kernel(tc, qT, k_words, k_scales, offs, out_0, out
         dealt = k_w[:].rearrange("p (r s) -> p s r", r=PACK)
         nc.vector.tensor_copy(dealt[:, : EARLY // PACK, :], pool_words[:, :PREFIX].indirect(offsets[:, : EARLY // 16]))
         nc.vector.tensor_copy(dealt[:, EARLY // PACK :, :], pool_words[:].indirect(offsets[:, EARLY // 16 :]))
-        for c in range(1, CHUNKS):
+        for c in range(1, len(Q_LOADS)):
             quantize_q(c)
 
         y_rows = out_0.rearrange("(p u) q -> p u q", u=PACK)
@@ -88,22 +88,24 @@ def tile_attend_plh_relu2_srt_kernel(tc, qT, k_words, k_scales, offs, out_0, out
         y_scales = sb.tile([P, NQ], U8, name="y_scales", align_bytes=64)
         acc = [[ps.tile([P, 2, CHUNK], F32, name="acc%d_%d" % (c, h)) for h in range(2)] if c in (0,) else
                [ps.tile([P, PACK, CHUNK], F32, name="acc%d" % c)] for c in range(CHUNKS)]
-        pos = []
+        pos_all = sb.tile([P, CHUNKS * PACK, CHUNK], F32, name="pos_all", tag="f32_3", align_bytes=64)
+        pos = [pos_all[:, c * PACK : (c + 1) * PACK, :] for c in range(CHUNKS)]
         y = [sb.tile([P, PACK, CHUNK], F32, name="y%d" % c, align_bytes=64) for c in range(CHUNKS)]
         y_bf = [sb.tile([P, CHUNK, PACK], BF16, name="y_bf%d" % c, align_bytes=64) for c in range(CHUNKS)]
 
         def multiply(c):
             per_bank = PACK // len(acc[c])
+            load = max(i for i, (first, n) in enumerate(Q_LOADS) if first <= c)
+            part = cols(c - Q_LOADS[load][0])
             for r in range(PACK):
                 slots = slice(r * P, (r + 1) * P)
                 nc.tensor.matmul_mx(out=acc[c][r // per_bank][:, r % per_bank, :], lhsT=k_w[:, slots].bitcast(FP8X4),
-                                    lhsT_scale=k_sc[:, slots], rhs=q_codes[c][:].bitcast(FP8X4),
-                                    rhs_scale=q_scales[c][:], start=True, stop=True)
+                                    lhsT_scale=k_sc[:, slots], rhs=q_codes[load][:, part].bitcast(FP8X4),
+                                    rhs_scale=q_scales[load][:, part], start=True, stop=True)
 
         def relu(c):
-            pos.append(sb.tile([P, PACK, CHUNK], F32, name="pos%d" % c, tag="f32_%d" % (CHUNKS - 1 - c), align_bytes=64))
             if len(acc[c]) == 1:
-                nc.scalar.activation(pos[c][:], acc[c][0][:], ACT.Relu)
+                nc.scalar.activation(pos[c], acc[c][0][:], ACT.Relu)
             else:
                 nc.scalar.activation(pos[c][:, 2:, :], acc[c][1][:], ACT.Relu)
                 nc.vector.tensor_scalar(pos[c][:, :2, :], acc[c][0][:], 0.0, None, ALU.max)

@@ -19,8 +19,7 @@ CHUNK = 128
 CHUNKS = NQ // CHUNK
 EARLY = N // 2
 PREFIX = T - (N - EARLY)
-VECTOR_SQUARES = (2, 4, 2, 0)
-Q_LOADS = [(0, 2), (2, 1), (3, 1)]
+HALF = NQ // 2
 FLOPS = 2 * D * N * NQ
 
 
@@ -34,40 +33,37 @@ def tile_attend_plh_relu2_srt_kernel(tc, qT, k_words, k_scales, offs, out_0, out
         sb = ctx.enter_context(tc.tile_pool(name="sb", bufs=1))
         ps = ctx.enter_context(tc.psum_pool(name="ps", bufs=1))
 
-        def cols(c, n=1):
-            return slice(c * CHUNK, (c + n) * CHUNK)
+        def half(h):
+            return slice(h * HALF, (h + 1) * HALF)
 
         q_rows = qT[0].rearrange("(p t) q -> p t q", t=PACK)
         words_in = k_words[0].rearrange("p n t -> p (n t)").bitcast(I32)
-        q_raw = [sb.tile([P, PACK, n * CHUNK], F32, name="q_raw%d" % c, tag="f32_%d" % c, align_bytes=64)
-                 for c, n in Q_LOADS]
+        q_raw = [sb.tile([P, PACK, HALF], F32, name="q_raw%d" % h, tag="f32_%d" % h, align_bytes=64) for h in range(2)]
         offsets = sb.tile([P, N // 16], U16, name="offsets", align_bytes=64)
         pool_words = sb.tile([P, T], U32, name="pool_words", align_bytes=64)
         pool_scales = sb.tile([P, T], U8, name="pool_scales", tag="scale_bytes", align_bytes=64)
 
         nc.vector.memset(pool_scales[:].bitcast(I32), 0)
-        nc.sync.dma_start(out=q_raw[0][:], in_=q_rows[:, :, cols(*Q_LOADS[0])])
+        nc.sync.dma_start(out=q_raw[0][:], in_=q_rows[:, :, half(0)])
         nc.sync.dma_start(offsets[:], offs)
         for quad in range(4):
             nc.sync.dma_start(out=pool_scales[32 * quad : 32 * quad + 4, :].bitcast(I32),
                               in_=k_scales[0, 4 * quad : 4 * quad + 4, :].bitcast(I32))
         nc.sync.dma_start(out=pool_words[:, :PREFIX].bitcast(I32), in_=words_in[:, :PREFIX])
         nc.sync.dma_start(out=pool_words[:, PREFIX:].bitcast(I32), in_=words_in[:, PREFIX:])
-        for i in range(1, len(Q_LOADS)):
-            nc.sync.dma_start(out=q_raw[i][:], in_=q_rows[:, :, cols(*Q_LOADS[i])])
+        nc.sync.dma_start(out=q_raw[1][:], in_=q_rows[:, :, half(1)])
 
-        q_bf = [sb.tile([P, n * CHUNK, PACK], BF16, name="q_bf%d" % c, align_bytes=64) for c, n in Q_LOADS]
-        q_codes = [sb.tile([P, n * CHUNK], U32, name="q_codes%d" % c, align_bytes=64) for c, n in Q_LOADS]
+        q_bf = [sb.tile([P, HALF, PACK], BF16, name="q_bf%d" % h, align_bytes=64) for h in range(2)]
+        q_codes = [sb.tile([P, HALF], U32, name="q_codes%d" % h, align_bytes=64) for h in range(2)]
         q_scales = []
 
-        def quantize_q(c):
-            tag = "scale_bytes" if c == 0 else "q_scales%d" % c
-            q_scales.append(sb.tile([P, Q_LOADS[c][1] * CHUNK], U8, name="q_scales%d" % c, tag=tag, align_bytes=64))
-            nc.vector.quantize_mx(out=q_codes[c][:].bitcast(FP8X4), scales=q_scales[c][:],
-                                  in_=q_bf[c][:].rearrange("p c t -> p (c t)"))
+        def quantize_q(h):
+            tag = "scale_bytes" if h == 0 else "q_scales1"
+            q_scales.append(sb.tile([P, HALF], U8, name="q_scales%d" % h, tag=tag, align_bytes=64))
+            nc.vector.quantize_mx(out=q_codes[h][:].bitcast(FP8X4), scales=q_scales[h][:],
+                                  in_=q_bf[h][:].rearrange("p c t -> p (c t)"))
 
-        for c in range(len(Q_LOADS)):
-            weave(nc.scalar.copy, q_bf[c][:], q_raw[c][:])
+        weave(nc.scalar.copy, q_bf[0][:], q_raw[0][:])
 
         listed_scales = sb.tile([P, N], U8, name="listed_scales", align_bytes=64)
         k_sc = sb.tile([P, N], U8, name="k_sc", align_bytes=64)
@@ -79,62 +75,83 @@ def tile_attend_plh_relu2_srt_kernel(tc, qT, k_words, k_scales, offs, out_0, out
         dealt = k_w[:].rearrange("p (r s) -> p s r", r=PACK)
         nc.vector.tensor_copy(dealt[:, : EARLY // PACK, :], pool_words[:, :PREFIX].indirect(offsets[:, : EARLY // 16]))
         nc.vector.tensor_copy(dealt[:, EARLY // PACK :, :], pool_words[:].indirect(offsets[:, EARLY // 16 :]))
-        for c in range(1, len(Q_LOADS)):
-            quantize_q(c)
+        weave(nc.scalar.copy, q_bf[1][:, :CHUNK, :], q_raw[1][:, :, :CHUNK])
+        weave(nc.vector.tensor_copy, q_bf[1][:, CHUNK:, :], q_raw[1][:, :, CHUNK:])
+        quantize_q(1)
 
         y_rows = out_0.rearrange("(p u) q -> p u q", u=PACK)
         y_words_out = out_1[0].rearrange("p q u -> p (q u)").bitcast(I32)
         y_codes = sb.tile([P, NQ], U32, name="y_codes", align_bytes=64)
         y_scales = sb.tile([P, NQ], U8, name="y_scales", align_bytes=64)
-        acc = [[ps.tile([P, 2, CHUNK], F32, name="acc%d_%d" % (c, h)) for h in range(2)] if c in (0,) else
-               [ps.tile([P, PACK, CHUNK], F32, name="acc%d" % c)] for c in range(CHUNKS)]
-        pos_all = sb.tile([P, CHUNKS * PACK, CHUNK], F32, name="pos_all", tag="f32_3", align_bytes=64)
-        pos = [pos_all[:, c * PACK : (c + 1) * PACK, :] for c in range(CHUNKS)]
-        y = [sb.tile([P, PACK, CHUNK], F32, name="y%d" % c, align_bytes=64) for c in range(CHUNKS)]
-        y_bf = [sb.tile([P, CHUNK, PACK], BF16, name="y_bf%d" % c, align_bytes=64) for c in range(CHUNKS)]
+        banks = [[(0, 1), (1, 1), (2, 1), (3, 1)], [(0, 2), (2, 1), (3, 1)]]
+        acc = {}
+        for h in range(2):
+            for first, n in banks[h]:
+                bank = ps.tile([P, n, HALF], F32, name="acc%d_%d" % (h, first))
+                acc[h, first] = bank
+                for r in range(first, first + n):
+                    slots = slice(r * P, (r + 1) * P)
+                    nc.tensor.matmul_mx(out=bank[:, r - first, :], lhsT=k_w[:, slots].bitcast(FP8X4),
+                                        lhsT_scale=k_sc[:, slots], rhs=q_codes[h][:].bitcast(FP8X4),
+                                        rhs_scale=q_scales[h][:], start=True, stop=True)
+        pos_all = sb.tile([P, 2 * PACK, HALF], F32, name="pos_all", tag="f32_1", align_bytes=64)
+        y = [sb.tile([P, PACK, HALF], F32, name="y%d" % h, align_bytes=64) for h in range(2)]
+        y_bf = [sb.tile([P, HALF, PACK], BF16, name="y_bf%d" % h, align_bytes=64) for h in range(2)]
 
-        def multiply(c):
-            per_bank = PACK // len(acc[c])
-            load = max(i for i, (first, n) in enumerate(Q_LOADS) if first <= c)
-            part = cols(c - Q_LOADS[load][0])
-            for r in range(PACK):
-                slots = slice(r * P, (r + 1) * P)
-                nc.tensor.matmul_mx(out=acc[c][r // per_bank][:, r % per_bank, :], lhsT=k_w[:, slots].bitcast(FP8X4),
-                                    lhsT_scale=k_sc[:, slots], rhs=q_codes[load][:, part].bitcast(FP8X4),
-                                    rhs_scale=q_scales[load][:, part], start=True, stop=True)
+        def pos(h, first, n):
+            return pos_all[:, h * PACK + first : h * PACK + first + n, :]
 
-        def relu(c):
-            if len(acc[c]) == 1:
-                nc.scalar.activation(pos[c], acc[c][0][:], ACT.Relu)
-            else:
-                nc.scalar.activation(pos[c][:, 2:, :], acc[c][1][:], ACT.Relu)
-                nc.vector.tensor_scalar(pos[c][:, :2, :], acc[c][0][:], 0.0, None, ALU.max)
+        def relu_v(h, first, n):
+            nc.vector.tensor_scalar(pos(h, first, n), acc[h, first][:], 0.0, None, ALU.max)
 
-        def square(c):
-            split = VECTOR_SQUARES[c]
-            if split > 0:
-                nc.vector.tensor_tensor(y[c][:, :split, :], pos[c][:, :split, :], pos[c][:, :split, :], ALU.mult)
-            if split < PACK:
-                nc.scalar.activation(y[c][:, split:, :], pos[c][:, split:, :], ACT.Square)
-            nc.sync.dma_start(out=y_rows[:, :, cols(c)], in_=y[c][:])
+        def relu_s(h, first, n):
+            nc.scalar.activation(pos(h, first, n), acc[h, first][:], ACT.Relu)
 
-        def round_y(c):
-            weave(nc.vector.tensor_copy, y_bf[c][:], y[c][:])
+        def square_v(h, first, n):
+            nc.vector.tensor_tensor(y[h][:, first : first + n, :], pos(h, first, n), pos(h, first, n), ALU.mult)
 
-        def quantize_y(c):
-            nc.vector.quantize_mx(out=y_codes[:, cols(c)].bitcast(FP8X4), scales=y_scales[:, cols(c)],
-                                  in_=y_bf[c][:].rearrange("p c t -> p (c t)"))
-            if c == 1:
-                nc.sync.dma_start(out=y_words_out[:, cols(0, c + 1)], in_=y_codes[:, cols(0, c + 1)].bitcast(I32))
-            if c == CHUNKS - 1:
-                rest = cols(1 + 1, CHUNKS - 1 - 1)
-                nc.sync.dma_start(out=y_words_out[:, rest], in_=y_codes[:, rest].bitcast(I32))
+        def square_s(h, first, n):
+            nc.scalar.activation(y[h][:, first : first + n, :], pos(h, first, n), ACT.Square)
 
-        stages = [multiply, relu, square, round_y, quantize_y]
-        for step in range(CHUNKS + len(stages) - 1):
-            for depth in range(len(stages)):
-                if 0 <= step - depth < CHUNKS:
-                    stages[depth](step - depth)
+        def store_y(h, first, n):
+            nc.sync.dma_start(out=y_rows[:, first : first + n, half(h)], in_=y[h][:, first : first + n, :])
+
+        def round_y(copy, h, lo, hi):
+            weave(copy, y_bf[h][:, lo:hi, :], y[h][:, :, lo:hi])
+
+        def quantize_y(h, lo, hi):
+            cols = slice(h * HALF + lo, h * HALF + hi)
+            nc.vector.quantize_mx(out=y_codes[:, cols].bitcast(FP8X4), scales=y_scales[:, cols],
+                                  in_=y_bf[h][:, lo:hi, :].rearrange("p c t -> p (c t)"))
+
+        def store_words(h):
+            nc.sync.dma_start(out=y_words_out[:, half(h)], in_=y_codes[:, half(h)].bitcast(I32))
+
+        relu_v(0, 0, 1)
+        relu_s(0, 1, 1)
+        square_v(0, 0, 1)
+        relu_s(0, 2, 1)
+        relu_v(0, 3, 1)
+        square_s(0, 1, 1)
+        store_y(0, 0, 2)
+        square_v(0, 2, 1)
+        square_s(0, 3, 1)
+        store_y(0, 2, 2)
+        relu_v(1, 0, 2)
+        relu_s(1, 2, 1)
+        relu_s(1, 3, 1)
+        round_y(nc.vector.tensor_copy, 0, 0, HALF)
+        square_s(1, 0, 2)
+        store_y(1, 0, 2)
+        square_v(1, 2, 1)
+        square_s(1, 3, 1)
+        store_y(1, 2, 2)
+        quantize_y(0, 0, HALF)
+        store_words(0)
+        round_y(nc.vector.tensor_copy, 1, 0, 160)
+        round_y(nc.scalar.copy, 1, 160, HALF)
+        quantize_y(1, 0, HALF)
+        store_words(1)
 
         for quad in range(4):
             queue = nc.scalar if quad % 2 == 0 else nc.sync

@@ -19,7 +19,9 @@ CHUNK = 128
 CHUNKS = NQ // CHUNK
 EARLY = N // 2
 PREFIX = T - (N - EARLY)
-HALF = NQ // 2
+RANGES = [(0, 256), (256, 256)]
+TAGS = {"q_scales0": "scale_bytes", "pos0_0": "f32_1", "pos0_2": "f32_2"}
+LOADS = [(0, 256), (256, 128), (384, 128)]
 FLOPS = 2 * D * N * NQ
 
 
@@ -33,125 +35,172 @@ def tile_attend_plh_relu2_srt_kernel(tc, qT, k_words, k_scales, offs, out_0, out
         sb = ctx.enter_context(tc.tile_pool(name="sb", bufs=1))
         ps = ctx.enter_context(tc.psum_pool(name="ps", bufs=1))
 
-        def half(h):
-            return slice(h * HALF, (h + 1) * HALF)
+        def cols(g, lo=0, hi=None):
+            first, width = RANGES[g]
+            return slice(first + lo, first + (width if hi is None else hi))
 
         q_rows = qT[0].rearrange("(p t) q -> p t q", t=PACK)
         words_in = k_words[0].rearrange("p n t -> p (n t)").bitcast(I32)
-        q_raw = [sb.tile([P, PACK, HALF], F32, name="q_raw%d" % h, tag="f32_%d" % h, align_bytes=64) for h in range(2)]
+        q_raw = [sb.tile([P, PACK, n], F32, name="q_raw%d" % g, tag="f32_%d" % g, align_bytes=64) for g, (first, n) in enumerate(LOADS)]
         offsets = sb.tile([P, N // 16], U16, name="offsets", align_bytes=64)
         pool_words = sb.tile([P, T], U32, name="pool_words", align_bytes=64)
         pool_scales = sb.tile([P, T], U8, name="pool_scales", tag="scale_bytes", align_bytes=64)
 
+        def load_words(lo, hi):
+            nc.sync.dma_start(out=pool_words[:, lo:hi].bitcast(I32), in_=words_in[:, lo:hi])
+
+        def load_scales(quad, queue):
+            queue.dma_start(out=pool_scales[32 * quad : 32 * quad + 4, :].bitcast(I32),
+                            in_=k_scales[0, 4 * quad : 4 * quad + 4, :].bitcast(I32))
+
+        def load_q(g):
+            nc.sync.dma_start(out=q_raw[g][:], in_=q_rows[:, :, LOADS[g][0] : LOADS[g][0] + LOADS[g][1]])
+
         nc.vector.memset(pool_scales[:].bitcast(I32), 0)
-        nc.sync.dma_start(out=q_raw[0][:], in_=q_rows[:, :, half(0)])
+        load_q(0)
         nc.sync.dma_start(offsets[:], offs)
-        for quad in range(4):
-            nc.sync.dma_start(out=pool_scales[32 * quad : 32 * quad + 4, :].bitcast(I32),
-                              in_=k_scales[0, 4 * quad : 4 * quad + 4, :].bitcast(I32))
-        nc.sync.dma_start(out=pool_words[:, :PREFIX].bitcast(I32), in_=words_in[:, :PREFIX])
-        nc.sync.dma_start(out=pool_words[:, PREFIX:].bitcast(I32), in_=words_in[:, PREFIX:])
-        nc.sync.dma_start(out=q_raw[1][:], in_=q_rows[:, :, half(1)])
-
-        q_bf = [sb.tile([P, HALF, PACK], BF16, name="q_bf%d" % h, align_bytes=64) for h in range(2)]
-        q_codes = [sb.tile([P, HALF], U32, name="q_codes%d" % h, align_bytes=64) for h in range(2)]
-        q_scales = []
-
-        def quantize_q(h):
-            tag = "scale_bytes" if h == 0 else "q_scales1"
-            q_scales.append(sb.tile([P, HALF], U8, name="q_scales%d" % h, tag=tag, align_bytes=64))
-            nc.vector.quantize_mx(out=q_codes[h][:].bitcast(FP8X4), scales=q_scales[h][:],
-                                  in_=q_bf[h][:].rearrange("p c t -> p (c t)"))
-
-        weave(nc.scalar.copy, q_bf[0][:], q_raw[0][:])
-
-        listed_scales = sb.tile([P, N], U8, name="listed_scales", align_bytes=64)
-        k_sc = sb.tile([P, N], U8, name="k_sc", align_bytes=64)
-        k_w = sb.tile([P, N], U32, name="k_w", align_bytes=64)
-        nc.vector.tensor_copy(listed_scales[:], pool_scales[:].indirect(offsets[:]))
-        quantize_q(0)
-        nc.vector.tensor_copy(k_sc[:].rearrange("p (r s) -> p r s", r=PACK),
-                              listed_scales[:].rearrange("p (s r) -> p r s", r=PACK))
-        dealt = k_w[:].rearrange("p (r s) -> p s r", r=PACK)
-        nc.vector.tensor_copy(dealt[:, : EARLY // PACK, :], pool_words[:, :PREFIX].indirect(offsets[:, : EARLY // 16]))
-        nc.vector.tensor_copy(dealt[:, EARLY // PACK :, :], pool_words[:].indirect(offsets[:, EARLY // 16 :]))
-        weave(nc.scalar.copy, q_bf[1][:, :CHUNK, :], q_raw[1][:, :, :CHUNK])
-        weave(nc.vector.tensor_copy, q_bf[1][:, CHUNK:, :], q_raw[1][:, :, CHUNK:])
-        quantize_q(1)
+        load_scales(0, nc.sync)
+        load_scales(1, nc.sync)
+        load_scales(2, nc.sync)
+        load_scales(3, nc.sync)
+        load_words(0, PREFIX)
+        load_words(PREFIX, T)
+        load_q(1)
+        load_q(2)
 
         y_rows = out_0.rearrange("(p u) q -> p u q", u=PACK)
         y_words_out = out_1[0].rearrange("p q u -> p (q u)").bitcast(I32)
+        tiles = {}
+
+        def tile(kind, g, shape, dtype):
+            if (kind, g) not in tiles:
+                name = "%s%d" % (kind, g)
+                tiles[kind, g] = sb.tile(shape, dtype, name=name, tag=TAGS.get(name, name), align_bytes=64)
+            return tiles[kind, g]
+
+        def q_bf(g):
+            return tile("q_bf", g, [P, CHUNK, PACK], BF16)
+
+        def q_codes(g):
+            return tile("q_codes", g, [P, RANGES[g][1]], U32)
+
+        def q_scales(g):
+            return tile("q_scales", g, [P, RANGES[g][1]], U8)
+
+        def pos(g, first, n, lo, hi):
+            if g == 1:
+                return tile("pos", 1, [P, PACK, 256], F32)[:, first : first + n, lo:hi]
+            base = first // 2 * 2
+            return tile("pos0_", base, [P, 2, 256], F32)[:, first - base : first - base + n, lo:hi]
+
+        def y(g):
+            return tile("y", g, [P, PACK, RANGES[g][1]], F32)
+
+        def y_bf(g):
+            return tile("y_bf", g, [P, RANGES[g][1], PACK], BF16)
+
+        listed_scales = sb.tile([P, N], U8, name="listed_scales", tag="listed", align_bytes=64)
+        k_w = sb.tile([P, N], U32, name="k_w", align_bytes=64)
         y_codes = sb.tile([P, NQ], U32, name="y_codes", align_bytes=64)
         y_scales = sb.tile([P, NQ], U8, name="y_scales", align_bytes=64)
-        banks = [[(0, 1), (1, 1), (2, 1), (3, 1)], [(0, 2), (2, 1), (3, 1)]]
+        dealt = k_w[:].rearrange("p (r s) -> p s r", r=PACK)
+        vcopy, scopy = nc.vector.tensor_copy, nc.scalar.copy
         acc = {}
-        for h in range(2):
-            for first, n in banks[h]:
-                bank = ps.tile([P, n, HALF], F32, name="acc%d_%d" % (h, first))
-                acc[h, first] = bank
-                for r in range(first, first + n):
-                    slots = slice(r * P, (r + 1) * P)
-                    nc.tensor.matmul_mx(out=bank[:, r - first, :], lhsT=k_w[:, slots].bitcast(FP8X4),
-                                        lhsT_scale=k_sc[:, slots], rhs=q_codes[h][:].bitcast(FP8X4),
-                                        rhs_scale=q_scales[h][:], start=True, stop=True)
-        pos_all = sb.tile([P, 2 * PACK, HALF], F32, name="pos_all", tag="f32_1", align_bytes=64)
-        y = [sb.tile([P, PACK, HALF], F32, name="y%d" % h, align_bytes=64) for h in range(2)]
-        y_bf = [sb.tile([P, HALF, PACK], BF16, name="y_bf%d" % h, align_bytes=64) for h in range(2)]
 
-        def pos(h, first, n):
-            return pos_all[:, h * PACK + first : h * PACK + first + n, :]
+        def gather_scales():
+            vcopy(listed_scales[:], pool_scales[:].indirect(offsets[:]))
 
-        def relu_v(h, first, n):
-            nc.vector.tensor_scalar(pos(h, first, n), acc[h, first][:], 0.0, None, ALU.max)
+        def deal_scales(first, n):
+            vcopy(tile("k_sc", 0, [P, N], U8)[:].rearrange("p (r s) -> p r s", r=PACK)[:, first : first + n, :],
+                  listed_scales[:].rearrange("p (s r) -> p r s", r=PACK)[:, first : first + n, :])
 
-        def relu_s(h, first, n):
-            nc.scalar.activation(pos(h, first, n), acc[h, first][:], ACT.Relu)
+        def gather_early():
+            vcopy(dealt[:, : EARLY // PACK, :], pool_words[:, :PREFIX].indirect(offsets[:, : EARLY // 16]))
 
-        def square_v(h, first, n):
-            nc.vector.tensor_tensor(y[h][:, first : first + n, :], pos(h, first, n), pos(h, first, n), ALU.mult)
+        def gather_late():
+            vcopy(dealt[:, EARLY // PACK :, :], pool_words[:].indirect(offsets[:, EARLY // 16 :]))
 
-        def square_s(h, first, n):
-            nc.scalar.activation(y[h][:, first : first + n, :], pos(h, first, n), ACT.Square)
+        def round_q(copy, g, lo, hi, key):
+            weave(copy, tile("q_bf", key[0], [P, key[1], PACK], BF16)[:, key[2] : key[2] + hi - lo, :], q_raw[g][:, :, lo:hi])
 
-        def store_y(h, first, n):
-            nc.sync.dma_start(out=y_rows[:, first : first + n, half(h)], in_=y[h][:, first : first + n, :])
+        def quantize_q(g, lo, hi, key):
+            nc.vector.quantize_mx(out=q_codes(g)[:, lo:hi].bitcast(FP8X4), scales=q_scales(g)[:, lo:hi],
+                                  in_=tiles["q_bf", key][:].rearrange("p c t -> p (c t)"))
 
-        def round_y(copy, h, lo, hi):
-            weave(copy, y_bf[h][:, lo:hi, :], y[h][:, :, lo:hi])
+        def multiply(g, first, n, lo=0, hi=256):
+            bank = ps.tile([P, n, hi - lo], F32, name="acc%d_%d_%d" % (g, first, lo))
+            acc[g, first, lo] = bank
+            for r in range(first, first + n):
+                slots = slice(r * P, (r + 1) * P)
+                nc.tensor.matmul_mx(out=bank[:, r - first, :], lhsT=k_w[:, slots].bitcast(FP8X4),
+                                    lhsT_scale=tile("k_sc", 0, [P, N], U8)[:, slots], rhs=q_codes(g)[:, lo:hi].bitcast(FP8X4),
+                                    rhs_scale=q_scales(g)[:, lo:hi], start=True, stop=True)
 
-        def quantize_y(h, lo, hi):
-            cols = slice(h * HALF + lo, h * HALF + hi)
-            nc.vector.quantize_mx(out=y_codes[:, cols].bitcast(FP8X4), scales=y_scales[:, cols],
-                                  in_=y_bf[h][:, lo:hi, :].rearrange("p c t -> p (c t)"))
+        def relu_v(g, first, n, lo=0, hi=256):
+            nc.vector.tensor_scalar(pos(g, first, n, lo, hi), acc[g, first, lo][:], 0.0, None, ALU.max)
 
-        def store_words(h):
-            nc.sync.dma_start(out=y_words_out[:, half(h)], in_=y_codes[:, half(h)].bitcast(I32))
+        def relu_s(g, first, n, lo=0, hi=256):
+            nc.scalar.activation(pos(g, first, n, lo, hi), acc[g, first, lo][:], ACT.Relu)
 
-        relu_v(0, 0, 1)
+        def square_v(g, first, n, lo=0, hi=256):
+            src = pos(g, first, n, lo, hi)
+            nc.vector.tensor_tensor(y(g)[:, first : first + n, lo:hi], src, src, ALU.mult)
+
+        def square_s(g, first, n, lo=0, hi=256):
+            nc.scalar.activation(y(g)[:, first : first + n, lo:hi], pos(g, first, n, lo, hi), ACT.Square)
+
+        def store_y(g, first, n, lo=0, hi=256):
+            nc.sync.dma_start(out=y_rows[:, first : first + n, cols(g, lo, hi)], in_=y(g)[:, first : first + n, lo:hi])
+
+        def round_y(copy, g, lo=0, hi=None):
+            weave(copy, y_bf(g)[:, lo:hi, :], y(g)[:, :, lo:hi])
+
+        def quantize_y(g, lo=0, hi=None):
+            nc.vector.quantize_mx(out=y_codes[:, cols(g, lo, hi)].bitcast(FP8X4), scales=y_scales[:, cols(g, lo, hi)],
+                                  in_=y_bf(g)[:, lo:hi, :].rearrange("p c t -> p (c t)"))
+
+        def store_words(lo, hi):
+            nc.sync.dma_start(out=y_words_out[:, lo:hi], in_=y_codes[:, lo:hi].bitcast(I32))
+
+        round_q(scopy, 0, 0, 256, (0, 256, 0))
+        gather_scales()
+        quantize_q(0, 0, 256, 0)
+        deal_scales(0, 4)
+        gather_early()
+        gather_late()
+        round_q(scopy, 1, 0, 128, (2, 128, 0))
+        round_q(vcopy, 2, 0, 128, (3, 128, 0))
+        quantize_q(1, 0, 128, 2)
+        quantize_q(1, 128, 256, 3)
+        multiply(0, 0, 1)
+        multiply(0, 1, 1)
+        multiply(0, 2, 1)
+        multiply(0, 3, 1)
+        multiply(1, 0, 4, 0, 128)
+        multiply(1, 0, 4, 128, 256)
+        relu_s(0, 0, 1)
         relu_s(0, 1, 1)
-        square_v(0, 0, 1)
         relu_s(0, 2, 1)
         relu_v(0, 3, 1)
-        square_s(0, 1, 1)
+        square_s(0, 0, 2)
         store_y(0, 0, 2)
-        square_v(0, 2, 1)
-        square_s(0, 3, 1)
+        square_v(0, 2, 2)
         store_y(0, 2, 2)
-        relu_v(1, 0, 2)
-        relu_s(1, 2, 1)
-        relu_s(1, 3, 1)
-        round_y(nc.vector.tensor_copy, 0, 0, HALF)
-        square_s(1, 0, 2)
-        store_y(1, 0, 2)
-        square_v(1, 2, 1)
-        square_s(1, 3, 1)
-        store_y(1, 2, 2)
-        quantize_y(0, 0, HALF)
-        store_words(0)
-        round_y(nc.vector.tensor_copy, 1, 0, 160)
-        round_y(nc.scalar.copy, 1, 160, HALF)
-        quantize_y(1, 0, HALF)
-        store_words(1)
+        relu_s(1, 0, 4, 0, 128)
+        round_y(vcopy, 0, 0, 128)
+        relu_s(1, 0, 4, 128, 256)
+        square_v(1, 0, 4, 0, 128)
+        store_y(1, 0, 4, 0, 128)
+        square_s(1, 0, 4, 128, 256)
+        store_y(1, 0, 4, 128, 256)
+        round_y(vcopy, 0, 128, 256)
+        round_y(vcopy, 1, 0, 128)
+        round_y(scopy, 1, 128, 256)
+        quantize_y(0)
+        store_words(0, 256)
+        quantize_y(1, 0, 128)
+        quantize_y(1, 128, 256)
+        store_words(256, 512)
 
         for quad in range(4):
             queue = nc.scalar if quad % 2 == 0 else nc.sync

@@ -20,7 +20,7 @@ CHUNKS = NQ // CHUNK
 EARLY = N // 2
 PREFIX = T - (N - EARLY)
 RANGES = [(0, 256), (256, 256)]
-TAGS = {"q_scales0": "scale_bytes", "pos0_0": "f32_1", "pos0_2": "f32_2"}
+TAGS = {"q_scales0": "scale_bytes", "pos0_0": "f32_1", "pos0_1": "f32_2", "pos0_2": "q_bf3", "pos0_3": "q_bf2", "pos1": "f32_2"}
 LOADS = [(0, 256), (256, 128), (384, 128)]
 FLOPS = 2 * D * N * NQ
 
@@ -90,8 +90,7 @@ def tile_attend_plh_relu2_srt_kernel(tc, qT, k_words, k_scales, offs, out_0, out
         def pos(g, first, n, lo, hi):
             if g == 1:
                 return tile("pos", 1, [P, PACK, 256], F32)[:, first : first + n, lo:hi]
-            base = first // 2 * 2
-            return tile("pos0_", base, [P, 2, 256], F32)[:, first - base : first - base + n, lo:hi]
+            return tile("pos0_", first, [P, 1, 256], F32)[:, :, lo:hi]
 
         def y(g):
             return tile("y", g, [P, PACK, RANGES[g][1]], F32)
@@ -179,25 +178,29 @@ def tile_attend_plh_relu2_srt_kernel(tc, qT, k_words, k_scales, offs, out_0, out
         multiply(1, 0, 4, 0, 128)
         multiply(1, 0, 4, 128, 256)
         relu_s(0, 0, 1)
-        relu_s(0, 1, 1)
-        relu_s(0, 2, 1)
+        relu_v(0, 1, 1)
+        relu_v(0, 2, 1)
+        square_s(0, 0, 1)
         relu_v(0, 3, 1)
-        square_s(0, 0, 2)
+        square_s(0, 1, 1)
         store_y(0, 0, 2)
-        square_v(0, 2, 2)
+        square_s(0, 2, 1)
+        square_v(0, 3, 1)
         store_y(0, 2, 2)
         relu_s(1, 0, 4, 0, 128)
         round_y(vcopy, 0, 0, 128)
         relu_s(1, 0, 4, 128, 256)
-        square_v(1, 0, 4, 0, 128)
+        square_v(1, 0, 3, 0, 128)
+        square_s(1, 3, 1, 0, 128)
         store_y(1, 0, 4, 0, 128)
         square_s(1, 0, 4, 128, 256)
         store_y(1, 0, 4, 128, 256)
         round_y(vcopy, 0, 128, 256)
         round_y(vcopy, 1, 0, 128)
-        round_y(scopy, 1, 128, 256)
+        round_y(scopy, 1, 160, 256)
         quantize_y(0)
         store_words(0, 256)
+        round_y(vcopy, 1, 128, 160)
         quantize_y(1, 0, 128)
         quantize_y(1, 128, 256)
         store_words(256, 512)

@@ -20,7 +20,7 @@ CHUNKS = NQ // CHUNK
 EARLY = N // 2
 PREFIX = T - (N - EARLY)
 RANGES = [(0, 256), (256, 256)]
-TAGS = {"q_scales0": "scale_bytes", "pos0_0": "f32_1", "pos0_1": "f32_2", "pos0_2": "q_bf3", "pos0_3": "q_bf2", "pos1": "f32_2"}
+TAGS = {"q_scales0": "scale_bytes", "pos0_0": "f32_1", "pos1_0": "f32_1", "pos0_2": "f32_2", "pos1_128": "f32_2", "pos0_3": "q_bf3"}
 LOADS = [(0, 256), (256, 128), (384, 128)]
 FLOPS = 2 * D * N * NQ
 
@@ -89,8 +89,10 @@ def tile_attend_plh_relu2_srt_kernel(tc, qT, k_words, k_scales, offs, out_0, out
 
         def pos(g, first, n, lo, hi):
             if g == 1:
-                return tile("pos", 1, [P, PACK, 256], F32)[:, first : first + n, lo:hi]
-            return tile("pos0_", first, [P, 1, 256], F32)[:, :, lo:hi]
+                return tile("pos1_", lo, [P, PACK, CHUNK], F32)[:, first : first + n, :]
+            if first < 2:
+                return tile("pos0_", 0, [P, 2, 256], F32)[:, first : first + n, :]
+            return tile("pos0_", first, [P, 1, 256], F32)[:]
 
         def y(g):
             return tile("y", g, [P, PACK, RANGES[g][1]], F32)
@@ -178,31 +180,30 @@ def tile_attend_plh_relu2_srt_kernel(tc, qT, k_words, k_scales, offs, out_0, out
         multiply(1, 0, 4, 0, 128)
         multiply(1, 0, 4, 128, 256)
         relu_s(0, 0, 1)
-        relu_v(0, 1, 1)
+        relu_s(0, 1, 1)
         relu_v(0, 2, 1)
         square_s(0, 0, 1)
         relu_v(0, 3, 1)
         square_s(0, 1, 1)
         store_y(0, 0, 2)
-        square_s(0, 2, 1)
+        square_v(0, 2, 1)
         square_v(0, 3, 1)
         store_y(0, 2, 2)
         relu_s(1, 0, 4, 0, 128)
-        round_y(vcopy, 0, 0, 128)
-        relu_s(1, 0, 4, 128, 256)
-        square_v(1, 0, 3, 0, 128)
-        square_s(1, 3, 1, 0, 128)
+        relu_v(1, 0, 4, 128, 256)
+        square_s(1, 0, 4, 0, 128)
         store_y(1, 0, 4, 0, 128)
+        round_y(vcopy, 0, 0, 128)
+        round_y(vcopy, 0, 128, 256)
         square_s(1, 0, 4, 128, 256)
         store_y(1, 0, 4, 128, 256)
-        round_y(vcopy, 0, 128, 256)
-        round_y(vcopy, 1, 0, 128)
-        round_y(scopy, 1, 160, 256)
-        quantize_y(0)
+        quantize_y(0, 0, 128)
+        round_y(scopy, 1, 0, 128)
+        round_y(vcopy, 1, 128, 256)
+        quantize_y(0, 128, 256)
         store_words(0, 256)
-        round_y(vcopy, 1, 128, 160)
-        quantize_y(1, 0, 128)
         quantize_y(1, 128, 256)
+        quantize_y(1, 0, 128)
         store_words(256, 512)
 
         for quad in range(4):

@@ -20,7 +20,7 @@ CHUNKS = NQ // CHUNK
 EARLY = N // 2
 PREFIX = T - (N - EARLY)
 RANGES = [(0, 256), (256, 256)]
-TAGS = {"q_scales0": "scale_bytes", "pos0_0": "f32_1", "pos1_0": "f32_1", "pos0_2": "f32_2", "pos1_128": "f32_2", "pos0_3": "q_bf3"}
+TAGS = {"q_scales0": "scale_bytes", "k_sc2": "word_bytes"}
 LOADS = [(0, 256), (256, 128), (384, 128)]
 FLOPS = 2 * D * N * NQ
 
@@ -33,6 +33,7 @@ def tile_attend_plh_relu2_srt_kernel(tc, qT, k_words, k_scales, offs, out_0, out
     nc = tc.nc
     with ExitStack() as ctx:
         sb = ctx.enter_context(tc.tile_pool(name="sb", bufs=1))
+        shared = ctx.enter_context(tc.tile_pool(name="shared", bufs=1))
         ps = ctx.enter_context(tc.psum_pool(name="ps", bufs=1))
 
         def cols(g, lo=0, hi=None):
@@ -41,9 +42,11 @@ def tile_attend_plh_relu2_srt_kernel(tc, qT, k_words, k_scales, offs, out_0, out
 
         q_rows = qT[0].rearrange("(p t) q -> p t q", t=PACK)
         words_in = k_words[0].rearrange("p n t -> p (n t)").bitcast(I32)
-        q_raw = [sb.tile([P, PACK, n], F32, name="q_raw%d" % g, tag="f32_%d" % g, align_bytes=64) for g, (first, n) in enumerate(LOADS)]
+        q_raw = [sb.tile([P, PACK, 256], F32, name="q_raw0", align_bytes=64),
+                 shared.tile([P, PACK, CHUNK], F32, name="q_raw1", offset=0),
+                 shared.tile([P, PACK, CHUNK], F32, name="q_raw2", offset=2048)]
         offsets = sb.tile([P, N // 16], U16, name="offsets", align_bytes=64)
-        pool_words = sb.tile([P, T], U32, name="pool_words", align_bytes=64)
+        pool_words = sb.tile([P, T], U32, name="pool_words", tag="word_bytes", align_bytes=64)
         pool_scales = sb.tile([P, T], U8, name="pool_scales", tag="scale_bytes", align_bytes=64)
 
         def load_words(lo, hi):
@@ -71,6 +74,7 @@ def tile_attend_plh_relu2_srt_kernel(tc, qT, k_words, k_scales, offs, out_0, out
         y_rows = out_0.rearrange("(p u) q -> p u q", u=PACK)
         y_words_out = out_1[0].rearrange("p q u -> p (q u)").bitcast(I32)
         tiles = {}
+        rows = {}
 
         def tile(kind, g, shape, dtype):
             if (kind, g) not in tiles:
@@ -88,11 +92,9 @@ def tile_attend_plh_relu2_srt_kernel(tc, qT, k_words, k_scales, offs, out_0, out
             return tile("q_scales", g, [P, RANGES[g][1]], U8)
 
         def pos(g, first, n, lo, hi):
-            if g == 1:
-                return tile("pos1_", lo, [P, PACK, CHUNK], F32)[:, first : first + n, :]
-            if first < 2:
-                return tile("pos0_", 0, [P, 2, 256], F32)[:, first : first + n, :]
-            return tile("pos0_", first, [P, 1, 256], F32)[:]
+            if (g, first) not in rows:
+                rows[g, first] = shared.tile([P, 1, 256], F32, name="pos%d_%d" % (g, first), offset=1024 * first)
+            return rows[g, first][:]
 
         def y(g):
             return tile("y", g, [P, PACK, RANGES[g][1]], F32)
@@ -112,7 +114,7 @@ def tile_attend_plh_relu2_srt_kernel(tc, qT, k_words, k_scales, offs, out_0, out
             vcopy(listed_scales[:], pool_scales[:].indirect(offsets[:]))
 
         def deal_scales(first, n):
-            vcopy(tile("k_sc", 0, [P, N], U8)[:].rearrange("p (r s) -> p r s", r=PACK)[:, first : first + n, :],
+            vcopy(tile("k_sc", first, [P, n * P], U8)[:].rearrange("p (r s) -> p r s", r=n),
                   listed_scales[:].rearrange("p (s r) -> p r s", r=PACK)[:, first : first + n, :])
 
         def gather_early():
@@ -134,7 +136,7 @@ def tile_attend_plh_relu2_srt_kernel(tc, qT, k_words, k_scales, offs, out_0, out
             for r in range(first, first + n):
                 slots = slice(r * P, (r + 1) * P)
                 nc.tensor.matmul_mx(out=bank[:, r - first, :], lhsT=k_w[:, slots].bitcast(FP8X4),
-                                    lhsT_scale=tile("k_sc", 0, [P, N], U8)[:, slots], rhs=q_codes(g)[:, lo:hi].bitcast(FP8X4),
+                                    lhsT_scale=tiles["k_sc", r // 2 * 2][:, r % 2 * P : (r % 2 + 1) * P], rhs=q_codes(g)[:, lo:hi].bitcast(FP8X4),
                                     rhs_scale=q_scales(g)[:, lo:hi], start=True, stop=True)
 
         def relu_v(g, first, n, lo=0, hi=256):
@@ -166,9 +168,10 @@ def tile_attend_plh_relu2_srt_kernel(tc, qT, k_words, k_scales, offs, out_0, out
         round_q(scopy, 0, 0, 256, (0, 256, 0))
         gather_scales()
         quantize_q(0, 0, 256, 0)
-        deal_scales(0, 4)
+        deal_scales(0, 2)
         gather_early()
         gather_late()
+        deal_scales(2, 2)
         round_q(scopy, 1, 0, 128, (2, 128, 0))
         round_q(vcopy, 2, 0, 128, (3, 128, 0))
         quantize_q(1, 0, 128, 2)
@@ -177,8 +180,10 @@ def tile_attend_plh_relu2_srt_kernel(tc, qT, k_words, k_scales, offs, out_0, out
         multiply(0, 1, 1)
         multiply(0, 2, 1)
         multiply(0, 3, 1)
-        multiply(1, 0, 4, 0, 128)
-        multiply(1, 0, 4, 128, 256)
+        multiply(1, 0, 1)
+        multiply(1, 1, 1)
+        multiply(1, 2, 1)
+        multiply(1, 3, 1)
         relu_s(0, 0, 1)
         relu_s(0, 1, 1)
         relu_v(0, 2, 1)
@@ -187,23 +192,27 @@ def tile_attend_plh_relu2_srt_kernel(tc, qT, k_words, k_scales, offs, out_0, out
         square_s(0, 1, 1)
         store_y(0, 0, 2)
         square_v(0, 2, 1)
+        relu_s(1, 0, 1)
         square_v(0, 3, 1)
         store_y(0, 2, 2)
-        relu_s(1, 0, 4, 0, 128)
-        relu_v(1, 0, 4, 128, 256)
-        square_s(1, 0, 4, 0, 128)
-        store_y(1, 0, 4, 0, 128)
+        relu_s(1, 1, 1)
+        relu_v(1, 2, 1)
+        square_s(1, 0, 1)
+        relu_v(1, 3, 1)
+        square_s(1, 1, 1)
+        store_y(1, 0, 2)
         round_y(vcopy, 0, 0, 128)
-        round_y(vcopy, 0, 128, 256)
-        square_s(1, 0, 4, 128, 256)
-        store_y(1, 0, 4, 128, 256)
+        square_s(1, 2, 1)
+        round_y(vcopy, 0, 128, 192)
+        square_s(1, 3, 1)
+        store_y(1, 2, 2)
         quantize_y(0, 0, 128)
-        round_y(scopy, 1, 0, 128)
-        round_y(vcopy, 1, 128, 256)
+        round_y(scopy, 0, 192, 256)
+        round_y(scopy, 1, 0, 96)
+        round_y(vcopy, 1, 96, 256)
         quantize_y(0, 128, 256)
         store_words(0, 256)
-        quantize_y(1, 128, 256)
-        quantize_y(1, 0, 128)
+        quantize_y(1)
         store_words(256, 512)
 
         for quad in range(4):

@@ -19,9 +19,8 @@ CHUNK = 128
 CHUNKS = NQ // CHUNK
 EARLY = N // 2
 PREFIX = T - (N - EARLY)
-RANGES = [(0, 256), (256, 256)]
-TAGS = {"q_scales0": "scale_bytes", "k_sc2": "word_bytes"}
-LOADS = [(0, 256), (256, 128), (384, 128)]
+TAGS = {"k_sc2": "word_bytes"}
+PLACES = {"q_raw1": 0, "pos0": 0}
 FLOPS = 2 * D * N * NQ
 
 
@@ -35,19 +34,28 @@ def tile_attend_plh_relu2_srt_kernel(tc, qT, k_words, k_scales, offs, out_0, out
         sb = ctx.enter_context(tc.tile_pool(name="sb", bufs=1))
         shared = ctx.enter_context(tc.tile_pool(name="shared", bufs=1))
         ps = ctx.enter_context(tc.psum_pool(name="ps", bufs=1))
+        tiles = {}
 
-        def cols(g, lo=0, hi=None):
-            first, width = RANGES[g]
-            return slice(first + lo, first + (width if hi is None else hi))
+        def tile(kind, g, shape, dtype):
+            name = "%s%d" % (kind, g)
+            if name not in tiles:
+                if name in PLACES:
+                    tiles[name] = shared.tile(shape, dtype, name=name, offset=PLACES[name], align_bytes=64)
+                else:
+                    tiles[name] = sb.tile(shape, dtype, name=name, tag=TAGS.get(name, name), align_bytes=64)
+            return tiles[name]
+
+        def cols(c, lo=0, hi=CHUNK):
+            return slice(c * CHUNK + lo, c * CHUNK + hi)
 
         q_rows = qT[0].rearrange("(p t) q -> p t q", t=PACK)
         words_in = k_words[0].rearrange("p n t -> p (n t)").bitcast(I32)
-        q_raw = [sb.tile([P, PACK, 256], F32, name="q_raw0", align_bytes=64),
-                 shared.tile([P, PACK, CHUNK], F32, name="q_raw1", offset=0),
-                 shared.tile([P, PACK, CHUNK], F32, name="q_raw2", offset=2048)]
         offsets = sb.tile([P, N // 16], U16, name="offsets", align_bytes=64)
         pool_words = sb.tile([P, T], U32, name="pool_words", tag="word_bytes", align_bytes=64)
         pool_scales = sb.tile([P, T], U8, name="pool_scales", tag="scale_bytes", align_bytes=64)
+
+        def q_raw(c):
+            return tile("q_raw", c, [P, PACK, CHUNK], F32)
 
         def load_words(lo, hi):
             nc.sync.dma_start(out=pool_words[:, lo:hi].bitcast(I32), in_=words_in[:, lo:hi])
@@ -56,53 +64,44 @@ def tile_attend_plh_relu2_srt_kernel(tc, qT, k_words, k_scales, offs, out_0, out
             queue.dma_start(out=pool_scales[32 * quad : 32 * quad + 4, :].bitcast(I32),
                             in_=k_scales[0, 4 * quad : 4 * quad + 4, :].bitcast(I32))
 
-        def load_q(g):
-            nc.sync.dma_start(out=q_raw[g][:], in_=q_rows[:, :, LOADS[g][0] : LOADS[g][0] + LOADS[g][1]])
+        def load_q(c):
+            nc.sync.dma_start(out=q_raw(c)[:], in_=q_rows[:, :, cols(c)])
 
         nc.vector.memset(pool_scales[:].bitcast(I32), 0)
         load_q(0)
         nc.sync.dma_start(offsets[:], offs)
-        load_scales(0, nc.sync)
+        load_scales(0, nc.scalar)
         load_scales(1, nc.sync)
-        load_scales(2, nc.sync)
+        load_scales(2, nc.scalar)
         load_scales(3, nc.sync)
         load_words(0, PREFIX)
         load_words(PREFIX, T)
         load_q(1)
         load_q(2)
+        load_q(3)
 
         y_rows = out_0.rearrange("(p u) q -> p u q", u=PACK)
         y_words_out = out_1[0].rearrange("p q u -> p (q u)").bitcast(I32)
-        tiles = {}
-        rows = {}
 
-        def tile(kind, g, shape, dtype):
-            if (kind, g) not in tiles:
-                name = "%s%d" % (kind, g)
-                tiles[kind, g] = sb.tile(shape, dtype, name=name, tag=TAGS.get(name, name), align_bytes=64)
-            return tiles[kind, g]
+        def q_bf(c):
+            return tile("q_bf", c, [P, CHUNK, PACK], BF16)
 
-        def q_bf(g):
-            return tile("q_bf", g, [P, CHUNK, PACK], BF16)
+        def q_codes(c):
+            return tile("q_codes", c, [P, CHUNK], U32)
 
-        def q_codes(g):
-            return tile("q_codes", g, [P, RANGES[g][1]], U32)
+        def q_scales(c):
+            return tile("q_scales", c, [P, CHUNK], U8)
 
-        def q_scales(g):
-            return tile("q_scales", g, [P, RANGES[g][1]], U8)
+        def pos(c, h):
+            return tile("pos", 2 * c + h, [P, 2, CHUNK], F32)
 
-        def pos(g, first, n, lo, hi):
-            if (g, first) not in rows:
-                rows[g, first] = shared.tile([P, 1, 256], F32, name="pos%d_%d" % (g, first), offset=1024 * first)
-            return rows[g, first][:]
+        def y(c):
+            return tile("y", c, [P, PACK, CHUNK], F32)
 
-        def y(g):
-            return tile("y", g, [P, PACK, RANGES[g][1]], F32)
+        def y_bf(c):
+            return tile("y_bf", c, [P, CHUNK, PACK], BF16)
 
-        def y_bf(g):
-            return tile("y_bf", g, [P, RANGES[g][1], PACK], BF16)
-
-        listed_scales = sb.tile([P, N], U8, name="listed_scales", tag="listed", align_bytes=64)
+        listed_scales = sb.tile([P, N], U8, name="listed_scales", align_bytes=64)
         k_w = sb.tile([P, N], U32, name="k_w", align_bytes=64)
         y_codes = sb.tile([P, NQ], U32, name="y_codes", align_bytes=64)
         y_scales = sb.tile([P, NQ], U8, name="y_scales", align_bytes=64)
@@ -113,9 +112,9 @@ def tile_attend_plh_relu2_srt_kernel(tc, qT, k_words, k_scales, offs, out_0, out
         def gather_scales():
             vcopy(listed_scales[:], pool_scales[:].indirect(offsets[:]))
 
-        def deal_scales(first, n):
-            vcopy(tile("k_sc", first, [P, n * P], U8)[:].rearrange("p (r s) -> p r s", r=n),
-                  listed_scales[:].rearrange("p (s r) -> p r s", r=PACK)[:, first : first + n, :])
+        def deal_scales(first):
+            vcopy(tile("k_sc", first, [P, 2 * P], U8)[:].rearrange("p (r s) -> p r s", r=2),
+                  listed_scales[:].rearrange("p (s r) -> p r s", r=PACK)[:, first : first + 2, :])
 
         def gather_early():
             vcopy(dealt[:, : EARLY // PACK, :], pool_words[:, :PREFIX].indirect(offsets[:, : EARLY // 16]))
@@ -123,96 +122,96 @@ def tile_attend_plh_relu2_srt_kernel(tc, qT, k_words, k_scales, offs, out_0, out
         def gather_late():
             vcopy(dealt[:, EARLY // PACK :, :], pool_words[:].indirect(offsets[:, EARLY // 16 :]))
 
-        def round_q(copy, g, lo, hi, key):
-            weave(copy, tile("q_bf", key[0], [P, key[1], PACK], BF16)[:, key[2] : key[2] + hi - lo, :], q_raw[g][:, :, lo:hi])
+        def round_q(copy, c, lo=0, hi=CHUNK):
+            weave(copy, q_bf(c)[:, lo:hi, :], q_raw(c)[:, :, lo:hi])
 
-        def quantize_q(g, lo, hi, key):
-            nc.vector.quantize_mx(out=q_codes(g)[:, lo:hi].bitcast(FP8X4), scales=q_scales(g)[:, lo:hi],
-                                  in_=tiles["q_bf", key][:].rearrange("p c t -> p (c t)"))
+        def quantize_q(c):
+            nc.vector.quantize_mx(out=q_codes(c)[:].bitcast(FP8X4), scales=q_scales(c)[:],
+                                  in_=q_bf(c)[:].rearrange("p c t -> p (c t)"))
 
-        def multiply(g, first, n, lo=0, hi=256):
-            bank = ps.tile([P, n, hi - lo], F32, name="acc%d_%d_%d" % (g, first, lo))
-            acc[g, first, lo] = bank
-            for r in range(first, first + n):
-                slots = slice(r * P, (r + 1) * P)
-                nc.tensor.matmul_mx(out=bank[:, r - first, :], lhsT=k_w[:, slots].bitcast(FP8X4),
-                                    lhsT_scale=tiles["k_sc", r // 2 * 2][:, r % 2 * P : (r % 2 + 1) * P], rhs=q_codes(g)[:, lo:hi].bitcast(FP8X4),
-                                    rhs_scale=q_scales(g)[:, lo:hi], start=True, stop=True)
+        def multiply(c):
+            for h in range(2):
+                bank = ps.tile([P, 2, CHUNK], F32, name="acc%d_%d" % (c, h))
+                acc[c, h] = bank
+                for i in range(2):
+                    r = 2 * h + i
+                    nc.tensor.matmul_mx(out=bank[:, i, :], lhsT=k_w[:, r * P : (r + 1) * P].bitcast(FP8X4),
+                                        lhsT_scale=tiles["k_sc%d" % (2 * h)][:, i * P : (i + 1) * P],
+                                        rhs=q_codes(c)[:].bitcast(FP8X4), rhs_scale=q_scales(c)[:], start=True, stop=True)
 
-        def relu_v(g, first, n, lo=0, hi=256):
-            nc.vector.tensor_scalar(pos(g, first, n, lo, hi), acc[g, first, lo][:], 0.0, None, ALU.max)
+        def relu_v(c, h):
+            nc.vector.tensor_scalar(pos(c, h)[:], acc[c, h][:], 0.0, None, ALU.max)
 
-        def relu_s(g, first, n, lo=0, hi=256):
-            nc.scalar.activation(pos(g, first, n, lo, hi), acc[g, first, lo][:], ACT.Relu)
+        def relu_s(c, h):
+            nc.scalar.activation(pos(c, h)[:], acc[c, h][:], ACT.Relu)
 
-        def square_v(g, first, n, lo=0, hi=256):
-            src = pos(g, first, n, lo, hi)
-            nc.vector.tensor_tensor(y(g)[:, first : first + n, lo:hi], src, src, ALU.mult)
+        def square_v(c, h):
+            nc.vector.tensor_tensor(y(c)[:, 2 * h : 2 * h + 2, :], pos(c, h)[:], pos(c, h)[:], ALU.mult)
 
-        def square_s(g, first, n, lo=0, hi=256):
-            nc.scalar.activation(y(g)[:, first : first + n, lo:hi], pos(g, first, n, lo, hi), ACT.Square)
+        def square_s(c, h):
+            nc.scalar.activation(y(c)[:, 2 * h : 2 * h + 2, :], pos(c, h)[:], ACT.Square)
 
-        def store_y(g, first, n, lo=0, hi=256):
-            nc.sync.dma_start(out=y_rows[:, first : first + n, cols(g, lo, hi)], in_=y(g)[:, first : first + n, lo:hi])
+        def store_y(c):
+            nc.sync.dma_start(out=y_rows[:, :, cols(c)], in_=y(c)[:])
 
-        def round_y(copy, g, lo=0, hi=None):
-            weave(copy, y_bf(g)[:, lo:hi, :], y(g)[:, :, lo:hi])
+        def round_y(copy, c, lo=0, hi=CHUNK):
+            weave(copy, y_bf(c)[:, lo:hi, :], y(c)[:, :, lo:hi])
 
-        def quantize_y(g, lo=0, hi=None):
-            nc.vector.quantize_mx(out=y_codes[:, cols(g, lo, hi)].bitcast(FP8X4), scales=y_scales[:, cols(g, lo, hi)],
-                                  in_=y_bf(g)[:, lo:hi, :].rearrange("p c t -> p (c t)"))
+        def quantize_y(c):
+            nc.vector.quantize_mx(out=y_codes[:, cols(c)].bitcast(FP8X4), scales=y_scales[:, cols(c)],
+                                  in_=y_bf(c)[:].rearrange("p c t -> p (c t)"))
 
         def store_words(lo, hi):
             nc.sync.dma_start(out=y_words_out[:, lo:hi], in_=y_codes[:, lo:hi].bitcast(I32))
 
-        round_q(scopy, 0, 0, 256, (0, 256, 0))
+        round_q(scopy, 0)
         gather_scales()
-        quantize_q(0, 0, 256, 0)
-        deal_scales(0, 2)
+        quantize_q(0)
+        deal_scales(0)
         gather_early()
         gather_late()
-        deal_scales(2, 2)
-        round_q(scopy, 1, 0, 128, (2, 128, 0))
-        round_q(vcopy, 2, 0, 128, (3, 128, 0))
-        quantize_q(1, 0, 128, 2)
-        quantize_q(1, 128, 256, 3)
-        multiply(0, 0, 1)
-        multiply(0, 1, 1)
-        multiply(0, 2, 1)
-        multiply(0, 3, 1)
-        multiply(1, 0, 1)
-        multiply(1, 1, 1)
-        multiply(1, 2, 1)
-        multiply(1, 3, 1)
-        relu_s(0, 0, 1)
-        relu_s(0, 1, 1)
-        relu_v(0, 2, 1)
-        square_s(0, 0, 1)
-        relu_v(0, 3, 1)
-        square_s(0, 1, 1)
-        store_y(0, 0, 2)
-        square_v(0, 2, 1)
-        relu_s(1, 0, 1)
-        square_v(0, 3, 1)
-        store_y(0, 2, 2)
-        relu_s(1, 1, 1)
-        relu_v(1, 2, 1)
-        square_s(1, 0, 1)
-        relu_v(1, 3, 1)
-        square_s(1, 1, 1)
-        store_y(1, 0, 2)
-        round_y(vcopy, 0, 0, 128)
-        square_s(1, 2, 1)
-        round_y(vcopy, 0, 128, 192)
-        square_s(1, 3, 1)
-        store_y(1, 2, 2)
-        quantize_y(0, 0, 128)
-        round_y(scopy, 0, 192, 256)
-        round_y(scopy, 1, 0, 96)
-        round_y(vcopy, 1, 96, 256)
-        quantize_y(0, 128, 256)
-        store_words(0, 256)
+        deal_scales(2)
+        multiply(0)
+        round_q(scopy, 1)
+        round_q(vcopy, 2)
+        quantize_q(1)
+        multiply(1)
+        relu_s(0, 0)
+        quantize_q(2)
+        multiply(2)
+        round_q(vcopy, 3)
+        relu_s(0, 1)
+        square_s(0, 0)
+        relu_v(1, 0)
+        quantize_q(3)
+        multiply(3)
+        square_s(0, 1)
+        store_y(0)
+        relu_s(1, 1)
+        relu_v(2, 0)
+        square_s(1, 0)
+        relu_v(2, 1)
+        square_s(1, 1)
+        store_y(1)
+        round_y(vcopy, 0)
+        relu_s(3, 0)
+        relu_v(3, 1)
+        square_s(2, 0)
+        square_v(2, 1)
+        store_y(2)
+        square_s(3, 0)
+        quantize_y(0)
+        square_s(3, 1)
+        store_y(3)
+        round_y(vcopy, 1)
+        round_y(scopy, 2, 0, 64)
+        round_y(vcopy, 2, 64, 128)
         quantize_y(1)
+        store_words(0, 256)
+        round_y(scopy, 3, 0, 48)
+        round_y(vcopy, 3, 48, 128)
+        quantize_y(2)
+        quantize_y(3)
         store_words(256, 512)
 
         for quad in range(4):

@@ -93,7 +93,8 @@ def tile_attend_plh_relu2_srt_kernel(tc, qT, k_words, k_scales, offs, out_0, out
             return tile("q_scales", c, [P, CHUNK], U8)
 
         def pos(c, h):
-            return tile("pos", 2 * c + h, [P, 2, CHUNK], F32)
+            return tile("pos", 2 * c + h, [P, 2, CHUNK], F32)[:]
+
 
         def y(c):
             return tile("y", c, [P, PACK, CHUNK], F32)
@@ -140,22 +141,28 @@ def tile_attend_plh_relu2_srt_kernel(tc, qT, k_words, k_scales, offs, out_0, out
                                         rhs=q_codes(c)[:].bitcast(FP8X4), rhs_scale=q_scales(c)[:], start=True, stop=True)
 
         def relu_v(c, h):
-            nc.vector.tensor_scalar(pos(c, h)[:], acc[c, h][:], 0.0, None, ALU.max)
+            nc.vector.tensor_scalar(pos(c, h), acc[c, h][:], 0.0, None, ALU.max)
 
         def relu_s(c, h):
-            nc.scalar.activation(pos(c, h)[:], acc[c, h][:], ACT.Relu)
+            nc.scalar.activation(pos(c, h), acc[c, h][:], ACT.Relu)
 
         def square_v(c, h):
-            nc.vector.tensor_tensor(y(c)[:, 2 * h : 2 * h + 2, :], pos(c, h)[:], pos(c, h)[:], ALU.mult)
+            nc.vector.tensor_tensor(y(c)[:, 2 * h : 2 * h + 2, :], pos(c, h), pos(c, h), ALU.mult)
+
+        def square_psum(c, h):
+            nc.vector.scalar_tensor_tensor(y(c)[:, 2 * h : 2 * h + 2, :], acc[c, h][:], 0.0, pos(c, h), ALU.max, ALU.mult)
 
         def square_s(c, h):
-            nc.scalar.activation(y(c)[:, 2 * h : 2 * h + 2, :], pos(c, h)[:], ACT.Square)
+            nc.scalar.activation(y(c)[:, 2 * h : 2 * h + 2, :], pos(c, h), ACT.Square)
 
-        def store_y(c):
-            nc.sync.dma_start(out=y_rows[:, :, cols(c)], in_=y(c)[:])
+        def store_y(c, first=0, last=PACK):
+            nc.sync.dma_start(out=y_rows[:, first:last, cols(c)], in_=y(c)[:, first:last, :])
 
         def round_y(copy, c, lo=0, hi=CHUNK):
             weave(copy, y_bf(c)[:, lo:hi, :], y(c)[:, :, lo:hi])
+
+        def round_y_pool(c, lo=0, hi=CHUNK):
+            nc.gpsimd.tensor_scalar(y_bf(c)[:, lo:hi, :], y(c)[:, :, lo:hi].rearrange("p t c -> p c t"), 1.0, 0.0, ALU.mult, ALU.add)
 
         def quantize_y(c):
             nc.vector.quantize_mx(out=y_codes[:, cols(c)].bitcast(FP8X4), scales=y_scales[:, cols(c)],
@@ -197,7 +204,7 @@ def tile_attend_plh_relu2_srt_kernel(tc, qT, k_words, k_scales, offs, out_0, out
         relu_s(3, 0)
         relu_v(3, 1)
         square_s(2, 0)
-        square_v(2, 1)
+        square_psum(2, 1)
         store_y(2)
         square_s(3, 0)
         quantize_y(0)

@@ -40,9 +40,9 @@ def tile_attend_plh_relu2_srt_kernel(tc, qT, k_words, k_scales, offs, out_0, out
             name = "%s%d" % (kind, g)
             if name not in tiles:
                 if name in PLACES:
-                    tiles[name] = shared.tile(shape, dtype, name=name, offset=PLACES[name], align_bytes=64)
+                    tiles[name] = shared.tile(shape, dtype, name=name, offset=PLACES[name], align_bytes=256)
                 else:
-                    tiles[name] = sb.tile(shape, dtype, name=name, tag=TAGS.get(name, name), align_bytes=64)
+                    tiles[name] = sb.tile(shape, dtype, name=name, tag=TAGS.get(name, name), align_bytes=256)
             return tiles[name]
 
         def cols(c, lo=0, hi=CHUNK):
@@ -50,9 +50,9 @@ def tile_attend_plh_relu2_srt_kernel(tc, qT, k_words, k_scales, offs, out_0, out
 
         q_rows = qT[0].rearrange("(p t) q -> p t q", t=PACK)
         words_in = k_words[0].rearrange("p n t -> p (n t)").bitcast(I32)
-        offsets = sb.tile([P, N // 16], U16, name="offsets", align_bytes=64)
-        pool_words = sb.tile([P, T], U32, name="pool_words", tag="word_bytes", align_bytes=64)
-        pool_scales = sb.tile([P, T], U8, name="pool_scales", tag="scale_bytes", align_bytes=64)
+        offsets = sb.tile([P, N // 16], U16, name="offsets", align_bytes=256)
+        pool_words = sb.tile([P, T], U32, name="pool_words", tag="word_bytes", align_bytes=256)
+        pool_scales = sb.tile([P, T], U8, name="pool_scales", tag="scale_bytes", align_bytes=256)
 
         def q_raw(c):
             return tile("q_raw", c, [P, PACK, CHUNK], F32)
@@ -102,10 +102,10 @@ def tile_attend_plh_relu2_srt_kernel(tc, qT, k_words, k_scales, offs, out_0, out
         def y_bf(c):
             return tile("y_bf", c, [P, CHUNK, PACK], BF16)
 
-        listed_scales = sb.tile([P, N], U8, name="listed_scales", align_bytes=64)
-        k_w = sb.tile([P, N], U32, name="k_w", align_bytes=64)
-        y_codes = sb.tile([P, NQ], U32, name="y_codes", align_bytes=64)
-        y_scales = sb.tile([P, NQ], U8, name="y_scales", align_bytes=64)
+        listed_scales = sb.tile([P, N], U8, name="listed_scales", align_bytes=256)
+        k_w = sb.tile([P, N], U32, name="k_w", align_bytes=256)
+        y_codes = sb.tile([P, NQ], U32, name="y_codes", align_bytes=256)
+        y_scales = sb.tile([P, NQ], U8, name="y_scales", align_bytes=256)
         dealt = k_w[:].rearrange("p (r s) -> p s r", r=PACK)
         vcopy, scopy = nc.vector.tensor_copy, nc.scalar.copy
         acc = {}
@@ -146,9 +146,6 @@ def tile_attend_plh_relu2_srt_kernel(tc, qT, k_words, k_scales, offs, out_0, out
         def relu_s(c, h):
             nc.scalar.activation(pos(c, h), acc[c, h][:], ACT.Relu)
 
-        def square_v(c, h):
-            nc.vector.tensor_tensor(y(c)[:, 2 * h : 2 * h + 2, :], pos(c, h), pos(c, h), ALU.mult)
-
         def square_psum(c, h):
             nc.vector.scalar_tensor_tensor(y(c)[:, 2 * h : 2 * h + 2, :], acc[c, h][:], 0.0, pos(c, h), ALU.max, ALU.mult)
 
@@ -160,9 +157,6 @@ def tile_attend_plh_relu2_srt_kernel(tc, qT, k_words, k_scales, offs, out_0, out
 
         def round_y(copy, c, lo=0, hi=CHUNK):
             weave(copy, y_bf(c)[:, lo:hi, :], y(c)[:, :, lo:hi])
-
-        def round_y_pool(c, lo=0, hi=CHUNK):
-            nc.gpsimd.tensor_scalar(y_bf(c)[:, lo:hi, :], y(c)[:, :, lo:hi].rearrange("p t c -> p c t"), 1.0, 0.0, ALU.mult, ALU.add)
 
         def quantize_y(c):
             nc.vector.quantize_mx(out=y_codes[:, cols(c)].bitcast(FP8X4), scales=y_scales[:, cols(c)],

@@ -19,8 +19,6 @@ CHUNK = 128
 CHUNKS = NQ // CHUNK
 EARLY = N // 2
 PREFIX = T - (N - EARLY)
-TAGS = {"k_sc2": "word_bytes"}
-PLACES = {"q_raw1": 0, "pos0": 0}
 FLOPS = 2 * D * N * NQ
 
 
@@ -32,17 +30,13 @@ def tile_attend_plh_relu2_srt_kernel(tc, qT, k_words, k_scales, offs, out_0, out
     nc = tc.nc
     with ExitStack() as ctx:
         sb = ctx.enter_context(tc.tile_pool(name="sb", bufs=1))
-        shared = ctx.enter_context(tc.tile_pool(name="shared", bufs=1))
         ps = ctx.enter_context(tc.psum_pool(name="ps", bufs=1))
         tiles = {}
 
         def tile(kind, g, shape, dtype):
             name = "%s%d" % (kind, g)
             if name not in tiles:
-                if name in PLACES:
-                    tiles[name] = shared.tile(shape, dtype, name=name, offset=PLACES[name], align_bytes=256)
-                else:
-                    tiles[name] = sb.tile(shape, dtype, name=name, tag=TAGS.get(name, name), align_bytes=256)
+                tiles[name] = sb.tile(shape, dtype, name=name, align_bytes=256)
             return tiles[name]
 
         def cols(c, lo=0, hi=CHUNK):
@@ -51,8 +45,8 @@ def tile_attend_plh_relu2_srt_kernel(tc, qT, k_words, k_scales, offs, out_0, out
         q_rows = qT[0].rearrange("(p t) q -> p t q", t=PACK)
         words_in = k_words[0].rearrange("p n t -> p (n t)").bitcast(I32)
         offsets = sb.tile([P, N // 16], U16, name="offsets", align_bytes=256)
-        pool_words = sb.tile([P, T], U32, name="pool_words", tag="word_bytes", align_bytes=256)
-        pool_scales = sb.tile([P, T], U8, name="pool_scales", tag="scale_bytes", align_bytes=256)
+        pool_words = sb.tile([P, T], U32, name="pool_words", align_bytes=256)
+        pool_scales = sb.tile([P, T], U8, name="pool_scales", align_bytes=256)
 
         def q_raw(c):
             return tile("q_raw", c, [P, PACK, CHUNK], F32)
@@ -103,6 +97,7 @@ def tile_attend_plh_relu2_srt_kernel(tc, qT, k_words, k_scales, offs, out_0, out
             return tile("y_bf", c, [P, CHUNK, PACK], BF16)
 
         listed_scales = sb.tile([P, N], U8, name="listed_scales", align_bytes=256)
+        k_sc = sb.tile([P, N], U8, name="k_sc", align_bytes=256)
         k_w = sb.tile([P, N], U32, name="k_w", align_bytes=256)
         y_codes = sb.tile([P, NQ], U32, name="y_codes", align_bytes=256)
         y_scales = sb.tile([P, NQ], U8, name="y_scales", align_bytes=256)
@@ -113,9 +108,8 @@ def tile_attend_plh_relu2_srt_kernel(tc, qT, k_words, k_scales, offs, out_0, out
         def gather_scales():
             vcopy(listed_scales[:], pool_scales[:].indirect(offsets[:]))
 
-        def deal_scales(first):
-            vcopy(tile("k_sc", first, [P, 2 * P], U8)[:].rearrange("p (r s) -> p r s", r=2),
-                  listed_scales[:].rearrange("p (s r) -> p r s", r=PACK)[:, first : first + 2, :])
+        def deal_scales():
+            vcopy(k_sc[:].rearrange("p (r s) -> p r s", r=PACK), listed_scales[:].rearrange("p (s r) -> p r s", r=PACK))
 
         def gather_early():
             vcopy(dealt[:, : EARLY // PACK, :], pool_words[:, :PREFIX].indirect(offsets[:, : EARLY // 16]))
@@ -126,9 +120,9 @@ def tile_attend_plh_relu2_srt_kernel(tc, qT, k_words, k_scales, offs, out_0, out
         def round_q(copy, c, lo=0, hi=CHUNK):
             weave(copy, q_bf(c)[:, lo:hi, :], q_raw(c)[:, :, lo:hi])
 
-        def quantize_q(c):
-            nc.vector.quantize_mx(out=q_codes(c)[:].bitcast(FP8X4), scales=q_scales(c)[:],
-                                  in_=q_bf(c)[:].rearrange("p c t -> p (c t)"))
+        def quantize_q(c, lo=0, hi=CHUNK):
+            nc.vector.quantize_mx(out=q_codes(c)[:, lo:hi].bitcast(FP8X4), scales=q_scales(c)[:, lo:hi],
+                                  in_=q_bf(c)[:, lo:hi, :].rearrange("p c t -> p (c t)"))
 
         def multiply(c):
             for h in range(2):
@@ -137,7 +131,7 @@ def tile_attend_plh_relu2_srt_kernel(tc, qT, k_words, k_scales, offs, out_0, out
                 for i in range(2):
                     r = 2 * h + i
                     nc.tensor.matmul_mx(out=bank[:, i, :], lhsT=k_w[:, r * P : (r + 1) * P].bitcast(FP8X4),
-                                        lhsT_scale=tiles["k_sc%d" % (2 * h)][:, i * P : (i + 1) * P],
+                                        lhsT_scale=k_sc[:, r * P : (r + 1) * P],
                                         rhs=q_codes(c)[:].bitcast(FP8X4), rhs_scale=q_scales(c)[:], start=True, stop=True)
 
         def relu_v(c, h):
@@ -146,7 +140,7 @@ def tile_attend_plh_relu2_srt_kernel(tc, qT, k_words, k_scales, offs, out_0, out
         def relu_s(c, h):
             nc.scalar.activation(pos(c, h), acc[c, h][:], ACT.Relu)
 
-        def square_psum(c, h):
+        def square_v(c, h):
             nc.vector.scalar_tensor_tensor(y(c)[:, 2 * h : 2 * h + 2, :], acc[c, h][:], 0.0, pos(c, h), ALU.max, ALU.mult)
 
         def square_s(c, h):
@@ -165,13 +159,15 @@ def tile_attend_plh_relu2_srt_kernel(tc, qT, k_words, k_scales, offs, out_0, out
         def store_words(lo, hi):
             nc.sync.dma_start(out=y_words_out[:, lo:hi], in_=y_codes[:, lo:hi].bitcast(I32))
 
-        round_q(scopy, 0)
+        round_q(vcopy, 0, 0, 64)
+        round_q(vcopy, 0, 64, 96)
+        round_q(scopy, 0, 96, 128)
+        quantize_q(0, 0, 64)
         gather_scales()
-        quantize_q(0)
-        deal_scales(0)
+        quantize_q(0, 64, 128)
+        deal_scales()
         gather_early()
         gather_late()
-        deal_scales(2)
         multiply(0)
         round_q(scopy, 1)
         round_q(vcopy, 2)
@@ -191,26 +187,26 @@ def tile_attend_plh_relu2_srt_kernel(tc, qT, k_words, k_scales, offs, out_0, out
         relu_s(1, 1)
         relu_v(2, 0)
         square_s(1, 0)
-        relu_v(2, 1)
+        round_y(vcopy, 0)
         square_s(1, 1)
         store_y(1)
-        round_y(vcopy, 0)
+        relu_v(2, 1)
         relu_s(3, 0)
         relu_v(3, 1)
         square_s(2, 0)
-        square_psum(2, 1)
-        store_y(2)
-        square_s(3, 0)
-        quantize_y(0)
-        square_s(3, 1)
-        store_y(3)
         round_y(vcopy, 1)
+        square_s(2, 1)
+        store_y(2)
+        square_v(3, 1)
+        square_s(3, 0)
+        store_y(3)
+        quantize_y(0)
         round_y(scopy, 2, 0, 64)
         round_y(vcopy, 2, 64, 128)
-        quantize_y(1)
-        store_words(0, 256)
         round_y(scopy, 3, 0, 48)
         round_y(vcopy, 3, 48, 128)
+        quantize_y(1)
+        store_words(0, 256)
         quantize_y(2)
         quantize_y(3)
         store_words(256, 512)

@@ -19,6 +19,7 @@ CHUNK = 128
 CHUNKS = NQ // CHUNK
 EARLY = N // 2
 PREFIX = T - (N - EARLY)
+TAGS = {"y_bf0": "pos4"}
 FLOPS = 2 * D * N * NQ
 
 
@@ -36,7 +37,7 @@ def tile_attend_plh_relu2_srt_kernel(tc, qT, k_words, k_scales, offs, out_0, out
         def tile(kind, g, shape, dtype):
             name = "%s%d" % (kind, g)
             if name not in tiles:
-                tiles[name] = sb.tile(shape, dtype, name=name, align_bytes=256)
+                tiles[name] = sb.tile(shape, dtype, name=name, tag=TAGS.get(name, name), align_bytes=256)
             return tiles[name]
 
         def cols(c, lo=0, hi=CHUNK):
@@ -140,9 +141,6 @@ def tile_attend_plh_relu2_srt_kernel(tc, qT, k_words, k_scales, offs, out_0, out
         def relu_s(c, h):
             nc.scalar.activation(pos(c, h), acc[c, h][:], ACT.Relu)
 
-        def square_v(c, h):
-            nc.vector.scalar_tensor_tensor(y(c)[:, 2 * h : 2 * h + 2, :], acc[c, h][:], 0.0, pos(c, h), ALU.max, ALU.mult)
-
         def square_s(c, h):
             nc.scalar.activation(y(c)[:, 2 * h : 2 * h + 2, :], pos(c, h), ACT.Square)
 
@@ -187,18 +185,18 @@ def tile_attend_plh_relu2_srt_kernel(tc, qT, k_words, k_scales, offs, out_0, out
         relu_s(1, 1)
         relu_v(2, 0)
         square_s(1, 0)
-        round_y(vcopy, 0)
+        relu_v(2, 1)
         square_s(1, 1)
         store_y(1)
-        relu_v(2, 1)
-        relu_s(3, 0)
-        relu_v(3, 1)
+        relu_v(3, 0)
         square_s(2, 0)
-        round_y(vcopy, 1)
+        relu_v(3, 1)
         square_s(2, 1)
         store_y(2)
-        square_v(3, 1)
+        round_y(vcopy, 0)
         square_s(3, 0)
+        round_y(vcopy, 1)
+        square_s(3, 1)
         store_y(3)
         quantize_y(0)
         round_y(scopy, 2, 0, 64)

@@ -19,7 +19,7 @@ CHUNK = 128
 CHUNKS = NQ // CHUNK
 EARLY = N // 2
 PREFIX = T - (N - EARLY)
-TAGS = {"y_bf0": "pos4"}
+TAGS = {"y_bf0": "pos3"}
 FLOPS = 2 * D * N * NQ
 
 
@@ -37,7 +37,7 @@ def tile_attend_plh_relu2_srt_kernel(tc, qT, k_words, k_scales, offs, out_0, out
         def tile(kind, g, shape, dtype):
             name = "%s%d" % (kind, g)
             if name not in tiles:
-                tiles[name] = sb.tile(shape, dtype, name=name, tag=TAGS.get(name, name), align_bytes=256)
+                tiles[name] = sb.tile(shape, dtype, name=name, tag=TAGS.get(name, name), align_bytes=512)
             return tiles[name]
 
         def cols(c, lo=0, hi=CHUNK):
@@ -45,9 +45,9 @@ def tile_attend_plh_relu2_srt_kernel(tc, qT, k_words, k_scales, offs, out_0, out
 
         q_rows = qT[0].rearrange("(p t) q -> p t q", t=PACK)
         words_in = k_words[0].rearrange("p n t -> p (n t)").bitcast(I32)
-        offsets = sb.tile([P, N // 16], U16, name="offsets", align_bytes=256)
-        pool_words = sb.tile([P, T], U32, name="pool_words", align_bytes=256)
-        pool_scales = sb.tile([P, T], U8, name="pool_scales", align_bytes=256)
+        offsets = sb.tile([P, N // 16], U16, name="offsets", align_bytes=512)
+        pool_words = sb.tile([P, T], U32, name="pool_words", align_bytes=512)
+        pool_scales = sb.tile([P, T], U8, name="pool_scales", align_bytes=512)
 
         def q_raw(c):
             return tile("q_raw", c, [P, PACK, CHUNK], F32)
@@ -97,20 +97,21 @@ def tile_attend_plh_relu2_srt_kernel(tc, qT, k_words, k_scales, offs, out_0, out
         def y_bf(c):
             return tile("y_bf", c, [P, CHUNK, PACK], BF16)
 
-        listed_scales = sb.tile([P, N], U8, name="listed_scales", align_bytes=256)
-        k_sc = sb.tile([P, N], U8, name="k_sc", align_bytes=256)
-        k_w = sb.tile([P, N], U32, name="k_w", align_bytes=256)
-        y_codes = sb.tile([P, NQ], U32, name="y_codes", align_bytes=256)
-        y_scales = sb.tile([P, NQ], U8, name="y_scales", align_bytes=256)
+        listed_scales = sb.tile([P, N], U8, name="listed_scales", align_bytes=512)
+        k_sc = sb.tile([P, N], U8, name="k_sc", align_bytes=512)
+        k_w = sb.tile([P, N], U32, name="k_w", align_bytes=512)
+        y_codes = sb.tile([P, NQ], U32, name="y_codes", align_bytes=512)
+        y_scales = sb.tile([P, NQ], U8, name="y_scales", align_bytes=512)
         dealt = k_w[:].rearrange("p (r s) -> p s r", r=PACK)
         vcopy, scopy = nc.vector.tensor_copy, nc.scalar.copy
         acc = {}
 
-        def gather_scales():
-            vcopy(listed_scales[:], pool_scales[:].indirect(offsets[:]))
+        def gather_scales(lo, hi):
+            vcopy(listed_scales[:, lo:hi], pool_scales[:].indirect(offsets[:, lo // 16 : hi // 16]))
 
-        def deal_scales():
-            vcopy(k_sc[:].rearrange("p (r s) -> p r s", r=PACK), listed_scales[:].rearrange("p (s r) -> p r s", r=PACK))
+        def deal_scales(lo, hi):
+            vcopy(k_sc[:].rearrange("p (r s) -> p r s", r=PACK)[:, :, lo // PACK : hi // PACK],
+                  listed_scales[:, lo:hi].rearrange("p (s r) -> p r s", r=PACK))
 
         def gather_early():
             vcopy(dealt[:, : EARLY // PACK, :], pool_words[:, :PREFIX].indirect(offsets[:, : EARLY // 16]))
@@ -161,9 +162,11 @@ def tile_attend_plh_relu2_srt_kernel(tc, qT, k_words, k_scales, offs, out_0, out
         round_q(vcopy, 0, 64, 96)
         round_q(scopy, 0, 96, 128)
         quantize_q(0, 0, 64)
-        gather_scales()
         quantize_q(0, 64, 128)
-        deal_scales()
+        gather_scales(0, EARLY)
+        gather_scales(EARLY, N)
+        deal_scales(0, EARLY)
+        deal_scales(EARLY, N)
         gather_early()
         gather_late()
         multiply(0)

@@ -19,7 +19,7 @@ CHUNK = 128
 CHUNKS = NQ // CHUNK
 EARLY = N // 2
 PREFIX = T - (N - EARLY)
-TAGS = {"y_bf0": "pos3"}
+TAGS = {"y_bf0": "pos4"}
 FLOPS = 2 * D * N * NQ
 
 
@@ -97,7 +97,6 @@ def tile_attend_plh_relu2_srt_kernel(tc, qT, k_words, k_scales, offs, out_0, out
         def y_bf(c):
             return tile("y_bf", c, [P, CHUNK, PACK], BF16)
 
-        listed_scales = sb.tile([P, N], U8, name="listed_scales", align_bytes=512)
         k_sc = sb.tile([P, N], U8, name="k_sc", align_bytes=512)
         k_w = sb.tile([P, N], U32, name="k_w", align_bytes=512)
         y_codes = sb.tile([P, NQ], U32, name="y_codes", align_bytes=512)
@@ -106,12 +105,8 @@ def tile_attend_plh_relu2_srt_kernel(tc, qT, k_words, k_scales, offs, out_0, out
         vcopy, scopy = nc.vector.tensor_copy, nc.scalar.copy
         acc = {}
 
-        def gather_scales(lo, hi):
-            vcopy(listed_scales[:, lo:hi], pool_scales[:].indirect(offsets[:, lo // 16 : hi // 16]))
-
-        def deal_scales(lo, hi):
-            vcopy(k_sc[:].rearrange("p (r s) -> p r s", r=PACK)[:, :, lo // PACK : hi // PACK],
-                  listed_scales[:, lo:hi].rearrange("p (s r) -> p r s", r=PACK))
+        def gather_scales():
+            vcopy(k_sc[:].rearrange("p (r s) -> p s r", r=PACK), pool_scales[:].indirect(offsets[:]))
 
         def gather_early():
             vcopy(dealt[:, : EARLY // PACK, :], pool_words[:, :PREFIX].indirect(offsets[:, : EARLY // 16]))
@@ -163,10 +158,7 @@ def tile_attend_plh_relu2_srt_kernel(tc, qT, k_words, k_scales, offs, out_0, out
         round_q(scopy, 0, 96, 128)
         quantize_q(0, 0, 64)
         quantize_q(0, 64, 128)
-        gather_scales(0, EARLY)
-        gather_scales(EARLY, N)
-        deal_scales(0, EARLY)
-        deal_scales(EARLY, N)
+        gather_scales()
         gather_early()
         gather_late()
         multiply(0)
@@ -179,33 +171,32 @@ def tile_attend_plh_relu2_srt_kernel(tc, qT, k_words, k_scales, offs, out_0, out
         multiply(2)
         round_q(vcopy, 3)
         relu_s(0, 1)
-        square_s(0, 0)
-        relu_v(1, 0)
         quantize_q(3)
         multiply(3)
+        square_s(0, 0)
+        relu_v(1, 0)
         square_s(0, 1)
         store_y(0)
-        relu_s(1, 1)
-        relu_v(2, 0)
+        relu_v(1, 1)
         square_s(1, 0)
-        relu_v(2, 1)
+        relu_v(2, 0)
         square_s(1, 1)
         store_y(1)
-        relu_v(3, 0)
+        relu_v(2, 1)
         square_s(2, 0)
-        relu_v(3, 1)
+        relu_v(3, 0)
         square_s(2, 1)
         store_y(2)
-        round_y(vcopy, 0)
+        relu_v(3, 1)
         square_s(3, 0)
-        round_y(vcopy, 1)
+        round_y(vcopy, 0)
         square_s(3, 1)
         store_y(3)
+        round_y(vcopy, 1)
+        round_y(scopy, 2)
         quantize_y(0)
-        round_y(scopy, 2, 0, 64)
-        round_y(vcopy, 2, 64, 128)
-        round_y(scopy, 3, 0, 48)
-        round_y(vcopy, 3, 48, 128)
+        round_y(scopy, 3, 0, 32)
+        round_y(vcopy, 3, 32, 128)
         quantize_y(1)
         store_words(0, 256)
         quantize_y(2)

@@ -19,7 +19,7 @@ CHUNK = 128
 CHUNKS = NQ // CHUNK
 EARLY = N // 2
 PREFIX = T - (N - EARLY)
-TAGS = {"y_bf0": "pos4"}
+TAGS = {"y_bf0": "pos4", "y_bf2": "pos6"}
 FLOPS = 2 * D * N * NQ
 
 
@@ -179,9 +179,10 @@ def tile_attend_plh_relu2_srt_kernel(tc, qT, k_words, k_scales, offs, out_0, out
         store_y(0)
         relu_v(1, 1)
         square_s(1, 0)
+        store_y(1, 0, 2)
         relu_v(2, 0)
         square_s(1, 1)
-        store_y(1)
+        store_y(1, 2, 4)
         relu_v(2, 1)
         square_s(2, 0)
         relu_v(3, 0)
@@ -193,10 +194,11 @@ def tile_attend_plh_relu2_srt_kernel(tc, qT, k_words, k_scales, offs, out_0, out
         square_s(3, 1)
         store_y(3)
         round_y(vcopy, 1)
-        round_y(scopy, 2)
+        round_y(scopy, 2, 0, 96)
+        round_y(vcopy, 2, 96, 128)
         quantize_y(0)
-        round_y(scopy, 3, 0, 32)
-        round_y(vcopy, 3, 32, 128)
+        round_y(scopy, 3, 0, 48)
+        round_y(vcopy, 3, 48, 128)
         quantize_y(1)
         store_words(0, 256)
         quantize_y(2)

from contextlib import ExitStack

import concourse.mybir as mybir

F32 = mybir.dt.float32
BF16 = mybir.dt.bfloat16
I32 = mybir.dt.int32
U32 = mybir.dt.uint32
U16 = mybir.dt.uint16
U8 = mybir.dt.uint8
FP8X4 = mybir.dt.float8_e4m3fn_x4
ACT = mybir.ActivationFunctionType
ALU = mybir.AluOpType

P = 128
PACK = 4
D, T, N, NQ = 512, 2048, 512, 512
CHUNK = 128
CHUNKS = NQ // CHUNK
EARLY = N // 2
PREFIX = T - (N - EARLY)
TAGS = {"y_bf0": "pos4", "y_bf2": "pos6"}
FLOPS = 2 * D * N * NQ


def weave(copy, dst, src):
    copy(dst.rearrange("p (c i) t -> p c t i", i=4), src.rearrange("p t (c i) -> p c t i", i=4))


def tile_attend_plh_relu2_srt_kernel(tc, qT, k_words, k_scales, offs, out_0, out_1, out_2):
    nc = tc.nc
    with ExitStack() as ctx:
        sb = ctx.enter_context(tc.tile_pool(name="sb", bufs=1))
        ps = ctx.enter_context(tc.psum_pool(name="ps", bufs=1))
        tiles = {}

        def tile(kind, g, shape, dtype):
            name = "%s%d" % (kind, g)
            if name not in tiles:
                tiles[name] = sb.tile(shape, dtype, name=name, tag=TAGS.get(name, name), align_bytes=512)
            return tiles[name]

        def cols(c, lo=0, hi=CHUNK):
            return slice(c * CHUNK + lo, c * CHUNK + hi)

        q_rows = qT[0].rearrange("(p t) q -> p t q", t=PACK)
        words_in = k_words[0].rearrange("p n t -> p (n t)").bitcast(I32)
        offsets = sb.tile([P, N // 16], U16, name="offsets", align_bytes=512)
        pool_words = sb.tile([P, T], U32, name="pool_words", align_bytes=512)
        pool_scales = sb.tile([P, T], U8, name="pool_scales", align_bytes=512)

        def q_raw(c):
            return tile("q_raw", c, [P, PACK, CHUNK], F32)

        def load_words(lo, hi):
            nc.sync.dma_start(out=pool_words[:, lo:hi].bitcast(I32), in_=words_in[:, lo:hi])

        def load_scales(quad, queue):
            queue.dma_start(out=pool_scales[32 * quad : 32 * quad + 4, :].bitcast(I32),
                            in_=k_scales[0, 4 * quad : 4 * quad + 4, :].bitcast(I32))

        def load_q(c):
            nc.sync.dma_start(out=q_raw(c)[:], in_=q_rows[:, :, cols(c)])

        nc.vector.memset(pool_scales[:].bitcast(I32), 0)
        load_q(0)
        nc.sync.dma_start(offsets[:], offs)
        load_scales(0, nc.scalar)
        load_scales(1, nc.sync)
        load_scales(2, nc.scalar)
        load_scales(3, nc.sync)
        load_words(0, PREFIX)
        load_words(PREFIX, T)
        load_q(1)
        load_q(2)
        load_q(3)

        y_rows = out_0.rearrange("(p u) q -> p u q", u=PACK)
        y_words_out = out_1[0].rearrange("p q u -> p (q u)").bitcast(I32)

        def q_bf(c):
            return tile("q_bf", c, [P, CHUNK, PACK], BF16)

        def q_codes(c):
            return tile("q_codes", c, [P, CHUNK], U32)

        def q_scales(c):
            return tile("q_scales", c, [P, CHUNK], U8)

        def pos(c, h):
            return tile("pos", 2 * c + h, [P, 2, CHUNK], F32)[:]


        def y(c):
            return tile("y", c, [P, PACK, CHUNK], F32)

        def y_bf(c):
            return tile("y_bf", c, [P, CHUNK, PACK], BF16)

        k_sc = sb.tile([P, N], U8, name="k_sc", align_bytes=512)
        k_w = sb.tile([P, N], U32, name="k_w", align_bytes=512)
        y_codes = sb.tile([P, NQ], U32, name="y_codes", align_bytes=512)
        y_scales = sb.tile([P, NQ], U8, name="y_scales", align_bytes=512)
        dealt = k_w[:].rearrange("p (r s) -> p s r", r=PACK)
        vcopy, scopy = nc.vector.tensor_copy, nc.scalar.copy
        acc = {}

        def gather_scales():
            vcopy(k_sc[:].rearrange("p (r s) -> p s r", r=PACK), pool_scales[:].indirect(offsets[:]))

        def gather_early():
            vcopy(dealt[:, : EARLY // PACK, :], pool_words[:, :PREFIX].indirect(offsets[:, : EARLY // 16]))

        def gather_late():
            vcopy(dealt[:, EARLY // PACK :, :], pool_words[:].indirect(offsets[:, EARLY // 16 :]))

        def round_q(copy, c, lo=0, hi=CHUNK):
            weave(copy, q_bf(c)[:, lo:hi, :], q_raw(c)[:, :, lo:hi])

        def quantize_q(c, lo=0, hi=CHUNK):
            nc.vector.quantize_mx(out=q_codes(c)[:, lo:hi].bitcast(FP8X4), scales=q_scales(c)[:, lo:hi],
                                  in_=q_bf(c)[:, lo:hi, :].rearrange("p c t -> p (c t)"))

        def multiply(c):
            for h in range(2):
                bank = ps.tile([P, 2, CHUNK], F32, name="acc%d_%d" % (c, h))
                acc[c, h] = bank
                for i in range(2):
                    r = 2 * h + i
                    nc.tensor.matmul_mx(out=bank[:, i, :], lhsT=k_w[:, r * P : (r + 1) * P].bitcast(FP8X4),
                                        lhsT_scale=k_sc[:, r * P : (r + 1) * P],
                                        rhs=q_codes(c)[:].bitcast(FP8X4), rhs_scale=q_scales(c)[:], start=True, stop=True)

        def relu_v(c, h):
            nc.vector.tensor_scalar(pos(c, h), acc[c, h][:], 0.0, None, ALU.max)

        def relu_s(c, h):
            nc.scalar.activation(pos(c, h), acc[c, h][:], ACT.Relu)

        def square_s(c, h):
            nc.scalar.activation(y(c)[:, 2 * h : 2 * h + 2, :], pos(c, h), ACT.Square)

        def store_y(c, first=0, last=PACK):
            nc.sync.dma_start(out=y_rows[:, first:last, cols(c)], in_=y(c)[:, first:last, :])

        def round_y(copy, c, lo=0, hi=CHUNK):
            weave(copy, y_bf(c)[:, lo:hi, :], y(c)[:, :, lo:hi])

        def quantize_y(c):
            nc.vector.quantize_mx(out=y_codes[:, cols(c)].bitcast(FP8X4), scales=y_scales[:, cols(c)],
                                  in_=y_bf(c)[:].rearrange("p c t -> p (c t)"))

        def store_words(lo, hi):
            nc.sync.dma_start(out=y_words_out[:, lo:hi], in_=y_codes[:, lo:hi].bitcast(I32))

        round_q(vcopy, 0, 0, 64)
        round_q(vcopy, 0, 64, 96)
        round_q(scopy, 0, 96, 128)
        quantize_q(0, 0, 64)
        quantize_q(0, 64, 128)
        gather_scales()
        gather_early()
        gather_late()
        multiply(0)
        round_q(scopy, 1)
        round_q(vcopy, 2)
        quantize_q(1)
        multiply(1)
        relu_s(0, 0)
        quantize_q(2)
        multiply(2)
        round_q(vcopy, 3)
        relu_s(0, 1)
        quantize_q(3)
        multiply(3)
        square_s(0, 0)
        relu_v(1, 0)
        square_s(0, 1)
        store_y(0)
        relu_v(1, 1)
        square_s(1, 0)
        store_y(1, 0, 2)
        relu_v(2, 0)
        square_s(1, 1)
        store_y(1, 2, 4)
        relu_v(2, 1)
        square_s(2, 0)
        relu_v(3, 0)
        square_s(2, 1)
        store_y(2)
        relu_v(3, 1)
        square_s(3, 0)
        round_y(vcopy, 0)
        square_s(3, 1)
        store_y(3)
        round_y(vcopy, 1)
        round_y(scopy, 2, 0, 96)
        round_y(vcopy, 2, 96, 128)
        quantize_y(0)
        round_y(scopy, 3, 0, 48)
        round_y(vcopy, 3, 48, 128)
        quantize_y(1)
        store_words(0, 256)
        quantize_y(2)
        quantize_y(3)
        store_words(256, 512)

        for quad in range(4):
            queue = nc.scalar if quad % 2 == 0 else nc.sync
            queue.dma_start(out=out_2[0, 4 * quad : 4 * quad + 4, :].bitcast(I32),
                            in_=y_scales[32 * quad : 32 * quad + 4, :].bitcast(I32))
